import numpy as np, ml_dtypes
CORES = [40,42,43,45,46]
N = 5
BF = ml_dtypes.bfloat16
def gentries(a):
    return np.ascontiguousarray(a.reshape(8, 16, -1).transpose(0, 2, 1)).reshape(8, -1)
def gtable(e):
    e = np.asarray(e); return np.ascontiguousarray(e.reshape(8, -1, 16).transpose(0, 2, 1)).reshape(128, -1).astype(np.int32)
W, TT, M, Q, SC = 2048, 1, 6, 4, 0.25
def tries(prev, cur, c):
    cs, ds = [], []
    for m in range(M):
        v = np.take_along_axis(prev, c[:, None, :], 2) - cur; d = np.add.reduce(v * v, axis=1)
        cs.append(c); ds.append(d); c = (5 * c + d + 1) & (W - 1)
    return np.stack(cs, axis=1), np.stack(ds, axis=1)
def parts(rng):
    return rng.integers(0, 16, (N, 8, 16, TT, W)), rng.integers(0, 16, (N, 8, 16, W)), rng.integers(0, 256, (N, 8, 16, W)), rng.integers(0, W, (N, 8, TT, W))
def walk(x, xb, c):
    d = np.zeros((N, 8, M, TT, W), np.int64); prev = xb[0]
    for r in range(N):
        for s in range(TT):
            cur = x[r, :, :, s]; d[r, :, :, s] = tries(prev, cur, c[r, :, s])[1]; prev = cur
    return d
def pack(x, xb, tb, c, th):
    return {"x": np.ascontiguousarray(x.reshape(N, 128, TT * W)).astype(np.float32).astype(BF), "xb": np.ascontiguousarray(xb.reshape(N, 128, W)).astype(np.float32).astype(BF),
            "tb": np.ascontiguousarray(tb.reshape(N, 128, W)).astype(np.float32).astype(BF),
            "c0": np.stack([gtable(a.reshape(8, -1)) for a in c]), "th": np.stack([gtable(a.reshape(8, -1)) for a in th])}
def setup_inputs(rng):
    x, xb, tb, c = parts(rng)
    th = rng.integers(350, 950, (N, 8, M, TT, W)) + rng.integers(-100, 101, (N, 8, 1, TT, 1))
    return pack(x, xb, tb, c, th)
def setup_inputs_ties(rng):
    x, xb, tb, c = parts(rng); d = walk(x, xb, c)
    return pack(x, xb, tb, c, np.clip(d + rng.integers(-1, 3, d.shape), 0, 4095))
def setup_inputs_counts(rng):
    x, xb, tb, c = parts(rng); d = walk(x, xb, c); a = rng.integers(0, 40, d.shape)
    p = rng.random(d.shape) < rng.random((N, 8, 1, TT, W))
    p[:, 0] = False; p[:, 1] = True; p[:, 2] = False; p[:, 2, M - 1] = True; p[:, 3] = False; p[:, 3, 0] = True
    return pack(x, xb, tb, c, np.where(p, np.minimum(d + 1 + a, 4095), np.maximum(d - a, 0)))
def setup_inputs_ends(rng):
    x, xb, tb, c = parts(rng); x = 15 * (x >> 3); xb = 15 * (xb >> 3); tb = 255 * (tb >> 7)
    even = ((np.arange(N * TT) & 1) == 0).reshape(N, 1, TT, 1)
    x[:, 5] = 15 * even; xb[:, 5] = 0; x[:, 6] = 0; xb[:, 6] = 0
    x[:, 3] = 15; xb[:, 3] = 15; tb[:, 3] = 255
    x[:, 2] = rng.integers(13, 16, (N, 16, TT, W)); xb[:, 2] = rng.integers(13, 16, (N, 16, W)); tb[:, 2] = rng.integers(240, 256, (N, 16, W))
    c = rng.choice(np.array([0, 1, W // 2, W - 1]), (N, 8, TT, W)); c[:, 4] = W - 1; c[:, 7] = 0; c[:, 2] = rng.integers(0, W, (N, TT, W))
    th = 225 * rng.integers(4, 13, (N, 8, M, TT, W)) + rng.integers(0, 2, (N, 8, M, TT, W))
    th[:, 5] = 3600 + rng.integers(0, 2, (N, M, TT, W)); th[:, 6] = rng.integers(0, 2, (N, M, TT, W)); th[:, 0, :, :, ::5] = 4095; th[:, 1, :, :, ::5] = 0
    th[:, 3] = rng.integers(0, 2, (N, M, TT, W)); th[:, 2] = rng.integers(10, 35, (N, M, TT, W))
    return pack(x, xb, tb, c, th)
def setup_inputs_alike(rng):
    x, xb, tb, c = parts(rng)
    x[:, ::2] = np.take_along_axis(rng.integers(0, 16, (N, 4, 16, TT, 8)), rng.integers(0, 8, (N, 4, 1, TT, W)), 4)
    c[:, 1] = rng.integers(0, W, (N, TT, 1)); c[:, 4] = rng.integers(0, W, (N, TT, 1))
    v = rng.integers(0, 15, 16); e = np.zeros(16, np.int64); e[rng.permutation(16)[:3]] = 1
    odd = (np.arange(N * TT) & 1).reshape(N, 1, TT, 1)
    x[:, 3] = v[None, :, None, None] + odd * e[None, :, None, None]; xb[:, 3] = (v + e)[None, :, None]
    same = (W // 8) * rng.integers(1, 9, (N, TT, W)) - 1
    c[:, 3] = np.where(rng.random((N, TT, W)) < 0.8, same, c[:, 3])
    d = walk(x, xb, c); th = np.clip(d + rng.integers(-60, 61, d.shape), 0, 4095)
    th[:, 3] = rng.integers(2, 6, (N, M, TT, W))
    return pack(x, xb, tb, c, th)
def setup_inputs_spread(rng):
    x, xb, tb, c = parts(rng)
    x = (np.exp2(rng.integers(0, 5, (N, 8, 1, TT, W))) * rng.random(x.shape)).astype(np.int64) * (rng.random((N, 8, 1, TT, W)) > 0.0625)
    xb = (np.exp2(rng.integers(0, 5, (N, 8, 1, W))) * rng.random(xb.shape)).astype(np.int64) * (rng.random((N, 8, 1, W)) > 0.0625)
    tb = np.minimum((np.exp2(8 * rng.random((N, 8, 1, W))) * rng.random(tb.shape)).astype(np.int64), 255)
    th = np.clip(np.exp2(12 * rng.random((N, 8, M, TT, W))).astype(np.int64) - 1, 0, 4095)
    return pack(x, xb, tb, c, th)
def check_inputs(d):
    bad = []
    for k, hi in (("x", 15), ("xb", 15), ("tb", 255), ("c0", W - 1), ("th", 4095)):
        v = np.asarray(d[k]).astype(np.float64)
        if np.min(v) < 0 or np.max(v) > hi: bad.append("range of " + k)
        if np.any(v != np.floor(v)): bad.append("whole numbers in " + k)
    return bad
def reference(x, xb, tb, c0, th):
    X = x.astype(np.float32).astype(np.int64).reshape(N, 8, 16, TT, W)
    prev = xb[0].astype(np.float32).astype(np.int64).reshape(8, 16, W); tau = tb[0].astype(np.float64).reshape(8, 16, W)
    C = np.stack([gentries(a) for a in c0]).astype(np.int64).reshape(N, 8, TT, W); H = np.stack([gentries(a) for a in th]).astype(np.int64).reshape(N, 8, M, TT, W)
    J = np.zeros((N, 8, Q, TT, W), np.int64); Y = []
    for r in range(N):
        for s in range(TT):
            cur = X[r, :, :, s]; cs, ds = tries(prev, cur, C[r, :, s])
            ok = ds < H[r, :, :, s]; n = np.add.accumulate(ok.astype(np.int64), axis=1)
            tot = np.zeros((8, 16, W))
            for q in range(Q):
                hit = ok & (n == q + 1)
                j = np.where(np.any(hit, axis=1), np.add.reduce(np.where(hit, cs, 0), axis=1), cs[:, M - 1])
                J[r, :, q, s] = j; tot = tot + np.take_along_axis(tau, j[:, None, :], 2)
            tau = tot * SC + cur; prev = cur
        Y.append(tau.reshape(128, W))
    return {"yj": np.stack([gtable(a.reshape(8, -1)) for a in J]).astype(np.float32), "ytau": np.stack(Y).astype(np.float32)}

@@ -1,0 +1,534 @@
+from concourse.bass import DstId, RemoteDMATransfer
+from concourse.mybir import AluOpType as OP
+from concourse.mybir import ActivationFunctionType as AF
+
+N = 5
+W = 2048
+WORKERS = [0, 2, 3, 4]
+WIN = 5648
+KEY = 8192
+BASE = 129 * W
+BIG = float(1 << 23)
+
+PAR = {
+    "load": [0, 1024, 2048],
+    "dve": [[[[18, 18, 14, 14]] * 2] * 5] * 5,
+    "steps": [["D2A2D2A2D2A2D2A2", "A2D2D2A1E1A2D2D2D2", "A2D2D2A2S2S2S2X2", "D2A2D2A2S2D2S2X2"]] * 4,
+    "fin": 128, "defer": [0, 2.5, 1.5, 13, 20],
+    "copy": [(0, 2048, 1024), (0, 4096, 1024), (1024, 3072, 1024), (1024, 5120, 528)],
+    "G": 1.55, "window": 0.0,
+}
+
+SCRATCH = {"XD": ("dram", [4, 128, 512], "bfloat16"), "TD": ("dram", [4, 128, 512], "bfloat16"), "XL": ("dram", [5, 128, 512], "bfloat16"),
+           "OD": ("dram", [8, 128, 256], "float32"), "LD": ("dram", [8, 128, 256], "float32")}
+for _d, _l in (("bfloat16", "X:2048 TAB:5648 ID:128 NID:128 N2:128 BB:144 LB:128 DIFF:2048 SQ:2048 GA:2048 HI:640 JK:512 TB:2048 XC:512 "
+                            "GH:2048 GL:2048 XR0:2048 XR1:2048 XR2:2048 XR3:2048"),
+               ("float32", "JR:608 JM:128 PF:8 L32:128 FF:136 I32:128 P5:128 N5:128 NB:128 CK:768 WS:256 AA:256 LT:512 YJ:512 FIN:512 "
+                           "G32:2048 T0:2048 T1:2048 T2:2048 T3:2048"),
+               ("float16", "TF:640 I16:128 WW:608 L16:128 JH:512 G16:2048"),
+               ("int32", "C0:128 TH:640 PI:8"), ("uint16", "OFF:640 JS:512 OFT:640")):
+    for _s in _l.split():
+        SCRATCH[_s.split(":")[0]] = ("sbuf", [128, int(_s.split(":")[1])], _d)
+for _b in range(8):
+    SCRATCH["PS%d" % _b] = ("psum", [128, 512], "float32")
+SEMAPHORES = ["cV", "cA", "cP", "cG"] + ["s%d" % _i for _i in range(120)]
+SIZE = {"bfloat16": 2, "float16": 2, "uint16": 2, "float32": 4, "int32": 4}
+IO = {"x": "bfloat16", "xb": "bfloat16", "tb": "bfloat16", "c0": "int32", "th": "int32", "yj": "float32", "ytau": "float32"}
+
+
+def ap(name, c0, c1, step=1, p0=0, p1=128, lead=None):
+    return (name, lead, p0, p1, c0, c1, step)
+
+
+def ind(win, off):
+    return ("*", win, off)
+
+
+def real(T, a):
+    if not isinstance(a, tuple):
+        return a
+    if a[0] == "*":
+        return real(T, a[1]).indirect(real(T, a[2]))
+    name, lead, p0, p1, c0, c1, step = a
+    if lead is not None:
+        if (p0, p1, c0, c1) == (0, 128, 0, SCRATCH[name][1][2]):
+            return T[name][lead]
+        return T[name][lead, p0:p1, c0:c1]
+    if step != 1:
+        return T[name][p0:p1, c0:c1:step]
+    return T[name][p0:p1, c0:c1]
+
+
+def width(a):
+    return (a[5] - a[4] + a[6] - 1) // a[6]
+
+
+def esize(a):
+    return SIZE[IO[a[0]] if a[0] in IO else SCRATCH[a[0]][2]]
+
+
+def in_psum(a):
+    return a[0].startswith("PS")
+
+
+def build(cores, topo):
+    CY, PE, G = 1.0, 0.5, PAR["G"]
+    nodes, seen, banks, pool, lead = [], {}, {}, [0] * N, [0.0]
+
+    def new_sem(r):
+        pool[r] += 1
+        return "s%d" % (pool[r] - 1)
+
+    def add(r, eng, emit, reads, writes, busy, lat=0.0, after=(), sem=None, gc=0):
+        i, deps = len(nodes), set(after)
+        flat = []
+        for a in reads:
+            flat += [(a[1], False), (a[2], False)] if a[0] == "*" else [(a, False)]
+        flat += [(a, True) for a in writes]
+        for a, wr in flat:
+            if a[0] in IO:
+                continue
+            for (b, bw, j) in seen.setdefault((r, a[0], a[1]), []):
+                if (wr or bw) and a[2] < b[3] and b[2] < a[3] and a[4] < b[5] and b[4] < a[5]:
+                    deps.add(j)
+        for name in set(a[0] for a, wr in flat if in_psum(a)):
+            st = banks.setdefault((r, name), [eng, [], []])
+            if st[0] != eng:
+                st[0], st[1], st[2] = eng, [], st[1]
+            st[1].append(i)
+            deps.update(st[2])
+        for a, wr in flat:
+            if a[0] not in IO:
+                seen[(r, a[0], a[1])].append((a, wr, i))
+        deps.discard(i)
+        nodes.append({"lead": lead[0], "r": r, "eng": eng, "emit": emit, "deps": deps, "busy": busy, "lat": lat, "sem": sem, "gc": gc})
+        return i
+
+    def vector(r, emit, out, ins, cols=(), two=False):
+        n = width(out)
+        if ins[0][0] == "*":
+            return add(r, "V", emit, ins + list(cols), [out], 50 + G * CY * n, 60, gc=n)
+        if two:
+            rate = 1 if any(in_psum(a) for a in ins) else 2
+        else:
+            rate = 0.5 if all(esize(a) == 2 for a in ins + [out]) else 1
+        return add(r, "V", emit, ins + list(cols), [out], max(64, n * rate) * CY + 10, 60)
+
+    def tt(r, out, a, b, op):
+        return vector(r, lambda g, T: g.vector.tensor_tensor(real(T, out), real(T, a), real(T, b), op), out, [a, b], two=True)
+
+    def ts(r, out, a, s1, s2, *ops):
+        return vector(r, lambda g, T: g.vector.tensor_scalar(real(T, out), real(T, a), real(T, s1), real(T, s2), *ops),
+                      out, [a], [s for s in (s1, s2) if isinstance(s, tuple)])
+
+    def cp(r, out, a):
+        return vector(r, lambda g, T: g.vector.tensor_copy(real(T, out), real(T, a)), out, [a])
+
+    def act(r, out, a, func=AF.Copy, scale=None, bias=None):
+        def emit(g, T):
+            if scale is None:
+                return g.scalar.activation(real(T, out), real(T, a), func)
+            return g.scalar.activation(real(T, out), real(T, a), func, bias=bias, scale=scale)
+        if a[0] == "*":
+            return add(r, "A", emit, [a], [out], 65 + G * CY * width(out), 60, gc=width(out))
+        return add(r, "A", emit, [a], [out], max(64, width(out)) * CY + 20, 60)
+
+    def mm(r, out, pairs, more=False, end=True):
+        def emit(g, T):
+            for n, (l, x) in enumerate(pairs):
+                last = g.tensor.matmul(real(T, out), real(T, l), real(T, x), n == 0 and not more, end and n == len(pairs) - 1)
+            return last
+        busy = sum(max(64, width(x)) * PE * (4 if esize(x) == 4 else 1) for l, x in pairs)
+        return add(r, "P", emit, [a for p in pairs for a in p], [out], busy, 100)
+
+    def iota(r, out, pattern, base, mult):
+        def emit(g, T):
+            if SCRATCH[out[0]][2] == "int32":
+                return g.iota(real(T, out), pattern, base, mult)
+            return g.iota(real(T, out), pattern, base, mult, allow_small_or_imprecise_dtypes=True)
+        return add(r, "G", emit, [], [out], 130 + 2 * CY * width(out), 60)
+
+    def dma(r, out, a, q="S", after=()):
+        nbytes = (a[3] - a[2]) * width(a) * esize(a)
+        return add(r, q, lambda g, T: (g.sync if q == "S" else g.scalar).dma_start(real(T, out), real(T, a)), [a], [out],
+                   60 + nbytes / 600.0, 1700 + nbytes / 300.0, after=after, sem=(new_sem(r), 16))
+
+    def send(r, moves, after=()):
+        share = 1
+        while 2 * share * len(moves) <= len(topo.engines(cores[r], cores[moves[0][0]])):
+            share *= 2
+        plan = []
+        for n, (d, out, a) in enumerate(moves):
+            e = topo.engines(cores[r], cores[d])
+            plan.append((d, out, a, sum(1 << v for v in e[n * share:(n + 1) * share]), new_sem(d)))
+        ls = new_sem(r)
+
+        def emit(g, T):
+            if len(plan) == 1:
+                d, out, a, m, s = plan[0]
+                rid, pid, se = topo.addr(cores[d])
+                g.remote_dma(real(T, out), real(T, a), T.sem[s], T.sem[ls], pid, rid, m)
+                return None
+            trs = []
+            for d, out, a, m, s in plan:
+                rid, pid, se = topo.addr(cores[d])
+                trs.append(RemoteDMATransfer(dst_ids=[DstId(rid=rid, pnc=pid)], dma_engine_mask=m, remote_sem=T.sem[s], src=real(T, a), dst=real(T, out)))
+            g.remote_dma_fused(trs, local_sem=T.sem[ls])
+            return None
+        srcs = [a for d, out, a in moves]
+        lat = 1500 + 128 * width(srcs[0]) * esize(srcs[0]) / (18.0 * share)
+        i = add(r, "G", emit, srcs, [], 700, 0, after=after, sem=("", 0))
+        for d, out, a, m, s in plan:
+            add(d, None, None, [], [out], 0, lat + 200, after=[i], sem=(s, share))
+        return add(r, None, None, srcs, [], 0, lat, after=[i], sem=(ls, share * len(moves)))
+
+    def turn(v):
+        lead[0] = -1e5 * v
+
+    col = lambda name, j: ap(name, j, j + 1)
+    mat = lambda name: ap(name, 0, 128)
+    gates = {}
+
+    for r in range(N):
+        cuts, ld, out = PAR["load"], [], []
+        turn(-2)
+        for a, b in zip(cuts, cuts[1:]):
+            ld.append(dma(r, ap("X", a, b), ap("x", a, b)))
+            if r + 1 < N:
+                out = [send(r, [(r + 1, ap("TAB", a, b), ap("X", a, b))])]
+        dma(r, mat("C0"), mat("c0"), q="A")
+        turn(-1)
+        if r == 0:
+            ld.append(dma(r, ap("TAB", 0, W), ap("xb", 0, W)))
+        turn(0)
+        dma(r, ap("TH", 0, 640), ap("th", 0, 640), after=ld)
+        gates[r] = ld + out
+    for r in range(N):
+        for a, b, n in PAR["copy"]:
+            gates[r].append(dma(r, ap("TAB", b, b + n), ap("xb" if r == 0 else "TAB", a, a + n), after=gates[r][:1] if r == 0 else ()))
+    for r in range(N):
+        iota(r, col("PI", 0), [[0, 1]], 0, 1)
+        iota(r, ap("JR", 0, 608), [[1, 608]], 0, 0)
+        cp(r, col("PF", 0), col("PI", 0))
+        for j, m in ((1, 31), (2, 112), (3, 96), (4, 32)):
+            ts(r, col("PI", j), col("PI", 0), m, None, OP.bitwise_and)
+        ts(r, col("PF", 2), col("PI", 2), 15.0, None, OP.add)
+        ts(r, ap("BB", 0, 144), ap("JR", 0, 144), col("PF", 2), None, OP.is_equal)
+        for name, v in (("ID", 1.0), ("I16", 1.0), ("NID", -1.0), ("I32", 1.0), ("N2", -2.0), ("P5", 5.0), ("N5", -5.0)):
+            ts(r, mat(name), mat("JR"), col("PF", 0), v, OP.is_equal, OP.mult)
+        ts(r, col("PF", 3), col("PI", 3), 3.0, col("PF", 0), OP.mult, OP.add)
+        ts(r, col("PF", 6), col("PF", 3), 96.0, None, OP.add)
+        ts(r, ap("WW", 0, 608), ap("JR", 0, 608), col("PF", 6), None, OP.is_equal)
+        if r in WORKERS:
+            iota(r, mat("JM"), [[0, 4], [1, 32]], 0, 0)
+            cp(r, col("PF", 1), col("PI", 1))
+            for name in ("L16", "LB", "L32"):
+                ts(r, mat(name), mat("JM"), col("PF", 1), 0.25, OP.is_equal, OP.mult)
+            ts(r, col("PF", 4), col("PI", 1), 4.0, 1.0, OP.mult, OP.add)
+            ts(r, col("PF", 5), col("PI", 4), 0.0625, col("PF", 4), OP.mult, OP.add)
+            ts(r, ap("FF", 0, 136), ap("JR", 0, 136), col("PF", 5), 0.25, OP.is_equal, OP.mult)
+
+    for r in range(N):
+        for src, stage, slot in ([("tb", "TD", 4)] if r == 0 else []) + [("x", "XD", r)]:
+            moves = []
+            for k, d in enumerate(WORKERS):
+                rows = lambda a, b: ap(src, a, b, p0=32 * k, p1=32 * k + 32)
+                if r == N - 1:
+                    for b in range(2):
+                        dst = ap("XC", 256 * b, 256 * b + 256) if d == r else ap(stage, 256 * b, 256 * b + 256, lead=k)
+                        dma(r, dst, rows(1024 * b, 1024 * b + 1024), after=gates[r])
+                    if d != r:
+                        moves.append((d, ap("XC", 0, 512), ap(stage, 0, 512, lead=k)))
+                elif d != r:
+                    dma(r, ap(stage, 0, 512, lead=k), rows(0, W), after=gates[r])
+                    moves.append((d, ap("XL", 0, 512, lead=slot), ap(stage, 0, 512, lead=k)))
+            send(r, moves)
+    for k, r in enumerate(WORKERS):
+        for slot, name, src, owner in [(4, "TB", "tb", 0)] + [(t, "XR%d" % t, "x", t) for t in range(4)]:
+            for q in range(4):
+                frm = ap(src, 0, W, p0=32 * k, p1=32 * k + 32) if owner == r else ap("XL", 0, 512, lead=slot)
+                dma(r, ap(name, 0, W, p0=32 * q, p1=32 * q + 32), frm, after=gates[r])
+
+    def blk(name, m, s):
+        return ap(name, 128 * m + 64 * s, 128 * m + 64 * s + 64)
+
+    defer = PAR["defer"]
+    for r in range(N):
+        turn(0)
+        for s in range(2):
+            cp(r, blk("OFF", 0, s), blk("C0", 0, s))
+        ts(r, mat("CK"), mat("C0"), float(BASE), None, OP.add)
+        for s in range(2):
+            n = max(sum(PAR["dve"][r][m][s][2:]) for m in range(5))
+            if n:
+                a, b = 1024 * s + 1024 - 16 * n, 1024 * s + 1024
+                act(r, ap("SQ", a, b), ap("X", a, b), AF.Square)
+                mm(r, ap("PS%d" % s, 0, n), [(ap("BB", 15 - p, 143 - p), ap("SQ", a + p, b, 16)) for p in range(16)])
+                act(r, ap("NB", 64 * s + 64 - n, 64 * s + 64), ap("PS%d" % s, 0, n))
+        for m in range(5):
+            turn(2 * m + 0.5)
+            ts(r, ap("TF", 128 * m, 128 * m + 128), ap("TH", 128 * m, 128 * m + 128), -1.0, 2048.0, OP.mult, OP.add)
+        for m in range(5):
+            for s in range(2):
+                o, x0, lc = 128 * m + 64 * s, 1024 * s, 0
+                tab = ap("TAB", 0, WIN if m else W)
+                pd, p2, pw, py = "PS%d" % s, "PS%d" % (2 + s), "PS%d" % (4 + s), "PS%d" % (6 + s)
+                turn(2 * m + s - 1)
+                act(r, blk("HI", m, s), blk("CK", m, s), AF.Identity, 5.0, -4.0 * BASE - 5.0 * KEY * m - 1022.5)
+                turn(2 * m + s)
+                mine, other = PAR["dve"][r][m][s][:2], PAR["dve"][r][m][s][2:]
+                u, fill = sum(mine), [0, 0]
+                rest = 64 - u - sum(other)
+                for j, n in [(0, min(16, rest - v)) for v in range(0, rest, 16)] + [(1, n) for n in other]:
+                    if n:
+                        a, b, h = x0 + 16 * u, x0 + 16 * (u + n), int(fill[1] < fill[0])
+                        ps = ap((p2, py)[h], fill[h], fill[h] + 16 * n)
+                        fill[h] += 16 * n
+                        mm(r, ps, [(mat("N2" if j else "NID"), ap("X", a, b))], end=False)
+                        act(r, ap("GA", a, b), ind(tab, ap("OFF", o + u, o + u + n)))
+                        mm(r, ps, [(mat("ID"), ap("GA", a, b))], more=True)
+                        if j:
+                            tt(r, ap("SQ", a, b), ps, ap("GA", a, b), OP.mult)
+                        else:
+                            act(r, ap("SQ", a, b), ps, AF.Square)
+                        u += n
+                for n in [n for n in mine if n]:
+                    a, b = x0 + 16 * lc, x0 + 16 * (lc + n)
+                    tt(r, ap("DIFF", a, b), ind(tab, ap("OFF", o + lc, o + lc + n)), ap("X", a, b), OP.subtract)
+                    act(r, ap("SQ", a, b), ap("DIFF", a, b), AF.Square)
+                    lc += n
+                d, ck = ap(pd, 0, 64), blk("CK", m + 1, s)
+                mm(r, d, [(mat("P5"), blk("CK", m, s)), (mat("NID"), blk("HI", m, s))], end=False)
+                if sum(other):
+                    mm(r, ap(pd, 64 - sum(other), 64), [(mat("I32"), ap("NB", 64 * s + 64 - sum(other), 64 * s + 64))], more=True, end=False)
+                mm(r, d, [(ap("BB", 15 - p, 143 - p), ap("SQ", x0 + p, x0 + 1024, 16)) for p in range(16)], more=True)
+                zero = 1.0 - 4 * BASE - 5 * KEY * m
+                if m < 4:
+                    ts(r, blk("OFF", m + 1, s), d, zero, None, OP.add)
+                turn(2 * m + s + (defer[0] if m < 4 else 0))
+                zero += BASE + KEY * (m + 1)
+                act(r, ck, d, AF.Identity, 1.0, zero)
+                mm(r, d, [(mat("N5"), blk("CK", m, s)), (mat("ID"), blk("HI", m, s)), (mat("I16"), blk("TF", m, s)), (mat("I32"), ck)])
+                act(r, ap(pw, 0, 64), d, AF.Identity, BIG, -(2047.5 + zero) * BIG)
+                turn(2 * m + s + (defer[1] if m < 4 else defer[2 + (r > 1)]))
+                ws = blk("WS", m // 2, s)
+                wp = ap(pw, 64, 128) if m < 4 else ap(pw, 320, 384)
+                tt(r, ws if m in (0, 2) else wp, ap(pw, 0, 64), blk("CK", m, s), OP.max)
+                lt = lambda j, n=1: ap("LT", 256 * s + 64 * j, 256 * s + 64 * (j + n))
+                if m == 1:
+                    tt(r, ap("AA", 128 * s, 128 * s + 64), wp, ws, OP.min)
+                    tt(r, ap("AA", 128 * s + 64, 128 * s + 128), wp, ws, OP.max)
+                if m == 3:
+                    aa = ap("AA", 128 * s, 128 * s + 128)
+                    tt(r, ap(pw, 128, 192), wp, ws, OP.min)
+                    tt(r, ap(pw, 192, 256), wp, ws, OP.max)
+                    tt(r, ap(pw, 256, 384), ap(pw, 128, 256), aa, OP.min)
+                    tt(r, lt(2, 2), ap(pw, 128, 256), aa, OP.max)
+                    tt(r, ap(pw, 384, 448), ap(pw, 320, 384), lt(2), OP.min)
+                    tt(r, ap(pw, 448, 512), ap(pw, 320, 384), lt(2), OP.max)
+                if m == 4:
+                    for j, a in enumerate((256, 384, 448)):
+                        tt(r, lt(j), ap(pw, a, a + 64), ck, OP.min)
+                    tt(r, ap(pw, 0, 64), wp, ck, OP.min)
+                    for j in range(3):
+                        tt(r, ap(pw, 64 * j + 64, 64 * j + 128), ap(pw, 0, 64), lt(j), OP.max)
+                    jb = lambda name, a=0, b=256: ap(name, 256 * s + a, 256 * s + b)
+                    keyed = ap(pw, 256, 512)
+                    tt(r, keyed, ap(pw, 0, 256), lt(0, 4), OP.min)
+                    act(r, jb("JK"), keyed, AF.Identity, 1.0, -1023.5)
+                    tt(r, jb("JH"), keyed, jb("JK"), OP.subtract)
+                    perm = lambda k, q: ap("WW", 128 * k + 96 - 32 * q, 128 * k + 224 - 32 * q)
+                    for k in range(4):
+                        if r < N - 1:
+                            mm(r, ap(py, 64 * k, 64 * k + 64), [(perm(k, q), jb("JH", 64 * q, 64 * q + 64)) for q in range(4)])
+                        else:
+                            for u in range(2):
+                                at = lambda q: 64 * (2 * (q // 2) + u) + 32 * (q % 2)
+                                mm(r, ap(py, 64 * k + 32 * u, 64 * k + 32 * u + 32), [(perm(k, q), jb("JH", at(q), at(q) + 32)) for q in range(4)])
+                    cp(r, jb("JS"), ap(py, 0, 256))
+                    send(r, [(d2, blk("OFT", r, s), jb("JS", 64 * k, 64 * k + 64)) for k, d2 in enumerate(WORKERS) if d2 != r])
+                    turn(30)
+                    mm(r, ap(pw, 0, 256), [(mat("I16"), jb("JH"))])
+                    for q in range(4):
+                        act(r, blk("YJ", q, s), ap(pw, 64 * q, 64 * q + 64))
+        turn(defer[4])
+        dma(r, ap("yj", 0, 512), ap("YJ", 0, 512))
+
+    def lists(r, t, a, b):
+        if t == r:
+            base = 256 * (a // 64) + 64 * WORKERS.index(r) + a % 64
+            return ap("JS", base, base + b - a)
+        return ap("OFT", 128 * t + a, 128 * t + b)
+
+    def piece(k, b):
+        return ap("ytau", 1024 * b, 1024 * b + 1024, p0=32 * k, p1=32 * k + 32)
+
+    for t in range(4):
+        for k, r in enumerate(WORKERS):
+            win = ap("TB" if t == 0 else "T%d" % (t - 1), 0, W)
+            plan, b = PAR["steps"][k][t], 0
+            for c in range(len(plan) // 2):
+                how, n = plan[2 * c], 128 * int(plan[2 * c + 1])
+                a, b = b, b + n
+                src = ind(win, lists(r, t, a // 16, b // 16))
+                ps = ap("PS%d" % (c % 4 if t == 0 else c % 8), 0, n)
+                xr, out = ap("XR%d" % t, a, b), ap("T%d" % t, a, b)
+                if how in "DE":
+                    gb = ap("G16" if t < 2 else "G32", a, b)
+                    tt(r, gb, src, xr, OP.add)
+                    pairs = [(mat("L16" if t < 2 else "L32"), gb)]
+                elif how in "AY":
+                    gb = ap("GH" if t == 0 else "G32", a, b)
+                    act(r, gb, src)
+                    pairs = [(mat("LB" if t == 0 else "L32"), gb)]
+                else:
+                    act(r, ap("GH", a, b), src)
+                    tt(r, ap("GL", a, b), src, ap("GH", a, b), OP.subtract)
+                    pairs = [(mat("LB"), ap("GH", a, b)), (mat("LB"), ap("GL", a, b))]
+                mm(r, ps, ([(mat("LB"), xr)] if how in "YX" else []) + pairs)
+                if how in "AS":
+                    tt(r, out, ps, xr, OP.add)
+                else:
+                    (cp if how == "E" else act)(r, out, ps)
+            for b in range(2):
+                rows = ap("T%d" % t, 1024 * b, 1024 * b + 1024, p1=32)
+                if r == t:
+                    dma(r, piece(k, b), rows)
+                else:
+                    dma(r, ap("OD", 0, 256, lead=2 * t + b), rows)
+                    send(r, [(t, ap("LD", 0, 256, lead=2 * k + b), ap("OD", 0, 256, lead=2 * t + b))])
+                    dma(t, piece(k, b), ap("LD", 0, 256, lead=2 * k + b))
+    t, n = N - 1, PAR["fin"]
+    for b in range(2):
+        for k, r in enumerate(WORKERS):
+            win = ap("T3", 0, W)
+            for c in range(0, 256, n):
+                pairs = [(mat("ID"), ap("XC", 256 * b + c, 256 * b + c + n))]
+                for jj in range(2):
+                    a, lc = 512 * b + 256 * jj + c, 64 * b + 16 * jj + c // 16
+                    act(r, ap("G32", a, a + n), ind(win, lists(r, t, lc, lc + n // 16)))
+                    tt(r, ap("G32", 1024 + a, 1024 + a + n), ind(win, lists(r, t, lc + 32, lc + 32 + n // 16)), ap("G32", a, a + n), OP.add)
+                    pairs.append((ap("FF", 1 - jj, 129 - jj), ap("G32", 1024 + a, 1024 + a + n)))
+                ps = ap("PS%d" % ((256 * b + c) // n % 8), 0, n)
+                mm(r, ps, pairs)
+                (cp if b == 1 and c + n == 256 else act)(r, ap("FIN", 256 * b + c, 256 * b + c + n), ps)
+            fin = ap("FIN", 256 * b, 256 * b + 256)
+            if r == t:
+                dma(r, piece(k, b), fin)
+            else:
+                send(r, [(t, ap("LD", 0, 256, lead=2 * k + b), fin)])
+                dma(t, piece(k, b), ap("LD", 0, 256, lead=2 * k + b), q="S" if k % 2 == 0 else "A")
+    return nodes
+
+
+def schedule(nodes):
+    HOP = 60.0
+    n = len(nodes)
+    users = [[] for _ in range(n)]
+    for i, v in enumerate(nodes):
+        for d in v["deps"]:
+            users[d].append(i)
+    way = [0.0] * n
+    for i in range(n - 1, -1, -1):
+        way[i] = nodes[i]["busy"] + nodes[i]["lat"] + max([way[u] + HOP for u in users[i]] + [0.0])
+    left = [len(v["deps"]) for v in nodes]
+    ready_at, done, start = [0.0] * n, [0.0] * n, [0.0] * n
+    free, ready, order = {}, {}, {}
+
+    def release(i):
+        v = nodes[i]
+        if v["eng"] is None:
+            finish(i, ready_at[i])
+        else:
+            ready.setdefault((v["r"], v["eng"]), []).append(i)
+
+    def finish(i, t0):
+        start[i] = t0
+        done[i] = t0 + nodes[i]["busy"] + nodes[i]["lat"]
+        for u in users[i]:
+            ready_at[u] = max(ready_at[u], done[i] + (HOP if nodes[u]["eng"] else 0.0))
+            left[u] -= 1
+            if left[u] == 0:
+                release(u)
+
+    for i in range(n):
+        if not nodes[i]["deps"]:
+            release(i)
+    while True:
+        best = None
+        for q, lst in ready.items():
+            if lst:
+                t0 = max(free.get(q, 0.0), min(ready_at[i] for i in lst))
+                if best is None or t0 < best[0]:
+                    best = (t0, q)
+        if best is None:
+            break
+        t0, q = best
+        i = max((i for i in ready[q] if ready_at[i] <= t0 + PAR["window"]), key=lambda i: (way[i] + nodes[i]["lead"], -i))
+        ready[q].remove(i)
+        t0 = max(t0, ready_at[i])
+        free[q] = t0 + nodes[i]["busy"]
+        order.setdefault(q, []).append(i)
+        finish(i, t0)
+    return order, start, done
+
+
+def waits(nodes, order, start):
+    mark = {}
+    for (r, eng), lst in order.items():
+        c = 0
+        for i in lst:
+            if nodes[i]["sem"] is None:
+                c += 1
+                mark[i] = ("c" + eng, c)
+    for i, v in enumerate(nodes):
+        if v["sem"] is not None:
+            mark[i] = v["sem"]
+    known, clock, need = {}, {}, {}
+    for i in sorted(range(len(nodes)), key=lambda i: (start[i], i)):
+        v = nodes[i]
+        if v["eng"] is None:
+            clock[i] = {}
+            continue
+        k = known.setdefault((v["r"], v["eng"]), {})
+        need[i] = {}
+        for d in sorted(v["deps"], key=lambda d: -start[d]):
+            name, c = mark[d]
+            if name and k.get(name, 0) < c and not (v["eng"] == "P" and name == "cP"):
+                need[i][name] = c
+                k[name] = c
+                for name2, c2 in clock[d].items():
+                    k[name2] = max(k.get(name2, 0), c2)
+        clock[i] = dict(k)
+    return mark, need
+
+
+PLAN = {}
+
+
+def rank_program(g, core, T, topo):
+    r = T.rank_of(core)
+    if r is None:
+        return
+    if not PLAN:
+        nodes = build(list(T.cores), topo)
+        order, start, done = schedule(nodes)
+        PLAN["all"] = (nodes, order, start, done) + waits(nodes, order, start)
+    nodes, order, start, done, mark, need = PLAN["all"]
+    queue = {"V": g.vector, "A": g.scalar, "P": g.tensor, "G": g, "S": g.sync}
+    top, got = {}, {}
+    for i, v in enumerate(nodes):
+        if v["r"] == r and mark[i][0]:
+            top[mark[i][0]] = max(top.get(mark[i][0], 0), mark[i][1])
+    mine = [i for (r2, eng), lst in order.items() if r2 == r for i in lst]
+    for i in sorted(mine, key=lambda i: (start[i], i)):
+        v = nodes[i]
+        for name, c in need[i].items():
+            queue[v["eng"]].wait_ge(T.sem[name], c)
+            got[name] = max(got.get(name, 0), c)
+        ins = v["emit"](g, T)
+        if ins is not None:
+            ins.then_inc(T.sem[mark[i][0]], 1 if v["sem"] is None else v["sem"][1])
+    for name, c in top.items():
+        if got.get(name, 0) < c:
+            g.wait_ge(T.sem[name], c)

@@ -8,24 +8,44 @@ WORKERS = [0, 2, 3, 4]
 WIN = 5648
 KEY = 8192
 BASE = 129 * W
-BIG = float(1 << 23)
+DOWN = 128.0
+UP = 4096.0
 
+COST = {"CY": 0.92, "PE": 0.46, "G": 1.56, "LAT": 0, "HOP": 200, "HS": 20, "DMA": 1820, "FAR": 850, "CALL": 130, "ROW": 12,
+        "FIRST": 600, "RATE": 1000, "RR": 780, "DD": 1, "VF": 33, "AF": 36, "MF": 5, "SI": 76}
+STEP2 = "A4S7D1S5A3D6D6 g6g5l1l3g2e4e1e3e0 g4h1h3g0e6e5e2 p4p6p5p1p3p0p2"
 PAR = {
-    "load": [0, 1024, 2048],
-    "dve": [[[[18, 18, 14, 14]] * 2] * 5] * 5,
-    "steps": [["D2A2D2A2D2A2D2A2", "A2D2D2A1E1A2D2D2D2", "A2D2D2A2S2S2S2X2", "D2A2D2A2S2D2S2X2"]] * 4,
-    "fin": 128, "defer": [0, 2.5, 1.5, 13, 20],
-    "copy": [(0, 2048, 1024), (0, 4096, 1024), (1024, 3072, 1024), (1024, 5120, 528)],
-    "G": 1.55, "window": 0.0,
+    "load": ["02 28 xb th"] + ["02 28 th"] * 4,
+    "mix": "V20V20M24",
+    "beat": ["o1m2v1w1", "r2g1c1h1q1", "s2a1z1p1"],
+    "steps": ["D8A8D4A4D4A4", "A2D6A4D4D6A4D4A2", STEP2, STEP2], "banks": "012301",
+    "fin": ["P128P128", "p128p128", "v0v1v2v3v4v5v6v7e2e3", "a0a1a2a3a4a5a6a7e0e1", "p0p1p2p3p4p5p6p7"],
+    "defer": [0, 2.5, 1.5, 20], "once": [0, 0, 1, 1, 1], "first": [10, 8, 0, 0, 0],
+    "parts": [[[0, 1, 2, 3]], [[2, 3], [0, 1]]],
+    "last": ["f ab g", "", "f ab g", "f g", "ab"],
 }
+LETTERS = "0123456789abcdefghijklmnopqrstuvwxyzABCDEFGHIJKLMNOPQRSTUVWXYZ+"
+ORDER = {
+    (0, "V"): "wxyzA014232lm33333333aba302102229923268867992256499584bb262829227562772234dd23bkk2aiv2t22r7225342297998777222233662564444233201000000110122311008713231108713231100000001100",
+    (0, "A"): "0000000114111522261222612226122261222612226132261222b19135241343111113642220020340000412021041202100011222200",
+    (0, "P"): "26000001131204112013120411201312240125011201716004442210001028304134100200211210004541200454120000000000",
+    (3, "V"): "wxyzA014232lm02a22222aba2221022555550200000022013312055140773607005340650012cb2aj0i08gon00010i00008098000100102012211001212110132321008713231108713231100000001100",
+    (3, "A"): "00000001103000411150111501115011150111501215012104210085632020211100234111351500100412021041202100011222200",
+    (3, "P"): "26000001131204112013120411204112013120411290116050442088893376001030000010213200104541200454120000000000",
+    (4, "V"): "wxyzA014232lm02a2928bcb42322210555550200000022013312055140773607005346050012cb2ak0i90g0mm101j034191108054033100243200001212110132321008713231108713231100000001100",
+    (4, "A"): "0000000000300041115011150111501115011150211503115012190504031023110023411135610010041202104120210001122220000",
+    (4, "P"): "26000001131204112013120411201312013125201201b1aa008824e012c01c00451125745144510010213200104541200454120000000000",
+}
+for _e in "VAP":
+    ORDER[(2, _e)] = ORDER[(3, _e)]
 
 SCRATCH = {"XD": ("dram", [4, 128, 512], "bfloat16"), "TD": ("dram", [4, 128, 512], "bfloat16"), "XL": ("dram", [5, 128, 512], "bfloat16"),
            "OD": ("dram", [8, 128, 256], "float32"), "LD": ("dram", [8, 128, 256], "float32")}
-for _d, _l in (("bfloat16", "X:2048 TAB:5648 ID:128 NID:128 N2:128 BB:144 LB:128 DIFF:2048 SQ:2048 GA:2048 HI:640 JK:512 TB:2048 XC:512 "
-                            "GH:2048 GL:2048 XR0:2048 XR1:2048 XR2:2048 XR3:2048"),
-               ("float32", "JR:608 JM:128 PF:8 L32:128 FF:136 I32:128 P5:128 N5:128 NB:128 CK:768 WS:256 AA:256 LT:512 YJ:512 FIN:512 "
+for _d, _l in (("bfloat16", "X:2048 TAB:5648 ID:128 N2:128 PU:128 NU:128 BB:144 LB:128 DIFF:2048 SQ:2048 GA:2048 HI:640 KC:320 JK:512 "
+                            "TB:2048 XC:512 GH:2048 GL:2048 XR0:2048 XR1:2048 XR2:2048 XR3:2048"),
+               ("float32", "JR:144 JM:128 PF:8 L32:128 FF:136 P5:128 N5:128 UD:128 CK:640 C4:512 WS:256 AA:256 LT:512 YJ:512 FIN:512 "
                            "G32:2048 T0:2048 T1:2048 T2:2048 T3:2048"),
-               ("float16", "TF:640 I16:128 WW:608 L16:128 JH:512 G16:2048"),
+               ("float16", "TF:640 U16:128 D16:128 NB:128 WW:608 L16:128 JH:512 G16:2048"),
                ("int32", "C0:128 TH:640 PI:8"), ("uint16", "OFF:640 JS:512 OFT:640")):
     for _s in _l.split():
         SCRATCH[_s.split(":")[0]] = ("sbuf", [128, int(_s.split(":")[1])], _d)
@@ -71,15 +91,29 @@ def in_psum(a):
     return a[0].startswith("PS")
 
 
+def in_sbuf(a):
+    return a[0] in SCRATCH and SCRATCH[a[0]][0] == "sbuf"
+
+
+def pieces(s):
+    out = []
+    for ch in s:
+        if ch.isdigit():
+            out[-1][1] = 10 * out[-1][1] + int(ch)
+        else:
+            out.append([ch, 0])
+    return [(a, b) for a, b in out if b]
+
+
 def build(cores, topo):
-    CY, PE, G = 1.0, 0.5, PAR["G"]
-    nodes, seen, banks, pool, lead = [], {}, {}, [0] * N, [0.0]
+    CY, PE, G, LAT = COST["CY"], COST["PE"], COST["G"], COST["LAT"]
+    nodes, seen, banks, pool, lead, tag, sent = [], {}, {}, [0] * N, [0.0], ["pre"], set()
 
     def new_sem(r):
         pool[r] += 1
         return "s%d" % (pool[r] - 1)
 
-    def add(r, eng, emit, reads, writes, busy, lat=0.0, after=(), sem=None, gc=0):
+    def add(r, eng, emit, reads, writes, busy, lat=0.0, after=(), sem=None):
         i, deps = len(nodes), set(after)
         flat = []
         for a in reads:
@@ -101,18 +135,20 @@ def build(cores, topo):
             if a[0] not in IO:
                 seen[(r, a[0], a[1])].append((a, wr, i))
         deps.discard(i)
-        nodes.append({"lead": lead[0], "r": r, "eng": eng, "emit": emit, "deps": deps, "busy": busy, "lat": lat, "sem": sem, "gc": gc})
+        name = "%s%d" % (writes[0][0], writes[0][4]) if writes else "send"
+        nodes.append({"lead": lead[0], "r": r, "eng": eng, "emit": emit, "deps": deps, "busy": busy, "lat": lat, "sem": sem,
+                      "tag": tag[0], "name": name, "soft": []})
         return i
 
     def vector(r, emit, out, ins, cols=(), two=False):
         n = width(out)
-        if ins[0][0] == "*":
-            return add(r, "V", emit, ins + list(cols), [out], 50 + G * CY * n, 60, gc=n)
+        if ins and ins[0][0] == "*":
+            return add(r, "V", emit, ins + list(cols), [out], 50 + G * CY * n, LAT)
         if two:
             rate = 1 if any(in_psum(a) for a in ins) else 2
         else:
             rate = 0.5 if all(esize(a) == 2 for a in ins + [out]) else 1
-        return add(r, "V", emit, ins + list(cols), [out], max(64, n * rate) * CY + 10, 60)
+        return add(r, "V", emit, ins + list(cols), [out], max(64, n * rate) * CY + COST["VF"], LAT)
 
     def tt(r, out, a, b, op):
         return vector(r, lambda g, T: g.vector.tensor_tensor(real(T, out), real(T, a), real(T, b), op), out, [a, b], two=True)
@@ -124,43 +160,53 @@ def build(cores, topo):
     def cp(r, out, a):
         return vector(r, lambda g, T: g.vector.tensor_copy(real(T, out), real(T, a)), out, [a])
 
-    def act(r, out, a, func=AF.Copy, scale=None, bias=None):
+    def const(r, out, v):
+        return vector(r, lambda g, T: g.vector.memset(real(T, out), v), out, [])
+
+    def act(r, out, a, func=AF.Copy, scale=None, bias=0.0):
         def emit(g, T):
             if scale is None:
                 return g.scalar.activation(real(T, out), real(T, a), func)
             return g.scalar.activation(real(T, out), real(T, a), func, bias=bias, scale=scale)
         if a[0] == "*":
-            return add(r, "A", emit, [a], [out], 65 + G * CY * width(out), 60, gc=width(out))
-        return add(r, "A", emit, [a], [out], max(64, width(out)) * CY + 20, 60)
+            return add(r, "A", emit, [a], [out], 65 + G * CY * width(out), LAT)
+        return add(r, "A", emit, [a], [out], max(64, width(out)) * CY + COST["AF"], LAT)
 
     def mm(r, out, pairs, more=False, end=True):
         def emit(g, T):
             for n, (l, x) in enumerate(pairs):
                 last = g.tensor.matmul(real(T, out), real(T, l), real(T, x), n == 0 and not more, end and n == len(pairs) - 1)
             return last
-        busy = sum(max(64, width(x)) * PE * (4 if esize(x) == 4 else 1) for l, x in pairs)
-        return add(r, "P", emit, [a for p in pairs for a in p], [out], busy, 100)
+        busy = sum(max(64, width(x)) * PE * (4 if esize(x) == 4 else 1) + COST["MF"] for l, x in pairs)
+        return add(r, "P", emit, [a for p in pairs for a in p], [out], busy, LAT + 40)
 
     def iota(r, out, pattern, base, mult):
         def emit(g, T):
             if SCRATCH[out[0]][2] == "int32":
                 return g.iota(real(T, out), pattern, base, mult)
             return g.iota(real(T, out), pattern, base, mult, allow_small_or_imprecise_dtypes=True)
-        return add(r, "G", emit, [], [out], 130 + 2 * CY * width(out), 60)
+        return add(r, "G", emit, [], [out], 130 + 2 * CY * width(out), LAT)
 
     def dma(r, out, a, q="S", after=()):
-        nbytes = (a[3] - a[2]) * width(a) * esize(a)
-        return add(r, q, lambda g, T: (g.sync if q == "S" else g.scalar).dma_start(real(T, out), real(T, a)), [a], [out],
-                   60 + nbytes / 600.0, 1700 + nbytes / 300.0, after=after, sem=(new_sem(r), 16))
+        sem = (new_sem(r), 16)
+        i = add(r, q, lambda g, T: (g.sync if q == "S" else g.scalar).dma_start(real(T, out), real(T, a)), [a], [out],
+                COST["SI"], 0, after=after, sem=("", 0))
+        nodes[i]["inc"] = sem
+        took = (a[3] - a[2]) * width(a) * esize(a) / COST["RATE"] * (1 if in_sbuf(a) or in_sbuf(out) else COST["DD"])
+        took += max(16, a[3] - a[2] if a[1] is None else out[3] - out[2]) * COST["ROW"] / 16
+        return add(r, "D", None, [a], [out], took, COST["DMA"], after=[i], sem=sem)
 
     def send(r, moves, after=()):
-        share = 1
-        while 2 * share * len(moves) <= len(topo.engines(cores[r], cores[moves[0][0]])):
-            share *= 2
+        have = len(topo.engines(cores[r], cores[moves[0][0]]))
+        shares = [1] * len(moves)
+        while 2 * sum(shares) <= have:
+            shares = [2 * v for v in shares]
+        if sum(shares) + shares[0] <= have:
+            shares[0] *= 2
         plan = []
         for n, (d, out, a) in enumerate(moves):
             e = topo.engines(cores[r], cores[d])
-            plan.append((d, out, a, sum(1 << v for v in e[n * share:(n + 1) * share]), new_sem(d)))
+            plan.append((d, out, a, sum(1 << v for v in e[sum(shares[:n]):sum(shares[:n + 1])]), new_sem(d)))
         ls = new_sem(r)
 
         def emit(g, T):
@@ -176,58 +222,88 @@ def build(cores, topo):
             g.remote_dma_fused(trs, local_sem=T.sem[ls])
             return None
         srcs = [a for d, out, a in moves]
-        lat = 1500 + 128 * width(srcs[0]) * esize(srcs[0]) / (18.0 * share)
-        i = add(r, "G", emit, srcs, [], 700, 0, after=after, sem=("", 0))
-        for d, out, a, m, s in plan:
-            add(d, None, None, [], [out], 0, lat + 200, after=[i], sem=(s, share))
-        return add(r, None, None, srcs, [], 0, lat, after=[i], sem=(ls, share * len(moves)))
+        took = [(128 * width(a) * esize(a) * 16 / COST["RR"] + (128 if in_sbuf(a) or in_sbuf(out) else c) * COST["ROW"]) / c
+                for (d, out, a), c in zip(moves, shares)]
+        i = add(r, "G", emit, srcs, [], COST["CALL"], 0.0 if r in sent else COST["FIRST"], after=after, sem=("", 0))
+        sent.add(r)
+        j = add(r, "D", None, [], [], max(took), 0, after=[i], sem=("", 0))
+        for (d, out, a, m, s), c in zip(plan, shares):
+            add(d, None, None, [], [out], 0, COST["FAR"] + 200, after=[j], sem=(s, c))
+        add(r, None, None, srcs, [], 0, COST["FAR"], after=[j], sem=(ls, sum(shares)))
+        return i
+
+    def gone(r):
+        return [i for i, v in enumerate(nodes) if v["r"] == r and v["eng"] is None and v["name"] == "send"][-1:]
+
+    def behind(i):
+        nodes[i]["soft"] += [j for j, v in enumerate(nodes[:i]) if (v["r"], v["eng"]) == (nodes[i]["r"], nodes[i]["eng"])]
 
     def turn(v):
         lead[0] = -1e5 * v
+
+    def follow(made, lists):
+        for lst in lists:
+            for j in range(2, len(lst), 2):
+                nodes[made[lst[j:j + 2]]]["soft"].append(made[lst[j - 2:j]])
 
     col = lambda name, j: ap(name, j, j + 1)
     mat = lambda name: ap(name, 0, 128)
     gates = {}
 
     for r in range(N):
-        cuts, ld, out = PAR["load"], [], []
+        ld, made = [], [len(nodes)]
         turn(-2)
-        for a, b in zip(cuts, cuts[1:]):
-            ld.append(dma(r, ap("X", a, b), ap("x", a, b)))
-            if r + 1 < N:
-                out = [send(r, [(r + 1, ap("TAB", a, b), ap("X", a, b))])]
         dma(r, mat("C0"), mat("c0"), q="A")
-        turn(-1)
-        if r == 0:
-            ld.append(dma(r, ap("TAB", 0, W), ap("xb", 0, W)))
-        turn(0)
-        dma(r, ap("TH", 0, 640), ap("th", 0, 640), after=ld)
-        gates[r] = ld + out
+        for what in PAR["load"][r].split():
+            made.append(len(nodes))
+            if what == "th":
+                dma(r, ap("TH", 0, 640), ap("th", 0, 640))
+            elif what == "xb":
+                ld.append(dma(r, ap("TAB", 0, W), ap("xb", 0, W)))
+            else:
+                a, b = [256 * int(v) for v in what]
+                ld.append(dma(r, ap("X", a, b), ap("x", a, b)))
+                if r + 1 < N:
+                    send(r, [(r + 1, ap("TAB", a, b), ap("X", a, b))])
+        for a, b in zip(made, made[1:]):
+            nodes[b]["soft"] += [a] if a != made[0] else []
+            nodes[b + 1]["soft"].append(a + 1)
+        gates[r] = ld + gone(r)
+    turn(0)
     for r in range(N):
-        for a, b, n in PAR["copy"]:
-            gates[r].append(dma(r, ap("TAB", b, b + n), ap("xb" if r == 0 else "TAB", a, a + n), after=gates[r][:1] if r == 0 else ()))
+        for a in (W, 2 * W) if r == 0 else ():
+            gates[r].append(dma(r, ap("TAB", a, min(a + W, WIN)), ap("xb", 0, min(W, WIN - a))))
+        for a in (W, 2 * W) if r + 1 < N else ():
+            behind(send(r, [(r + 1, ap("TAB", a, min(a + W, WIN)), ap("X", 0, min(W, WIN - a)))]))
+        gates[r] += gone(r)
     for r in range(N):
         iota(r, col("PI", 0), [[0, 1]], 0, 1)
-        iota(r, ap("JR", 0, 608), [[1, 608]], 0, 0)
+        iota(r, ap("JR", 0, 144), [[1, 144]], 0, 0)
         cp(r, col("PF", 0), col("PI", 0))
-        for j, m in ((1, 31), (2, 112), (3, 96), (4, 32)):
+        for j, m in ((1, 31), (2, 112), (4, 32)):
             ts(r, col("PI", j), col("PI", 0), m, None, OP.bitwise_and)
         ts(r, col("PF", 2), col("PI", 2), 15.0, None, OP.add)
-        ts(r, ap("BB", 0, 144), ap("JR", 0, 144), col("PF", 2), None, OP.is_equal)
-        for name, v in (("ID", 1.0), ("I16", 1.0), ("NID", -1.0), ("I32", 1.0), ("N2", -2.0), ("P5", 5.0), ("N5", -5.0)):
-            ts(r, mat(name), mat("JR"), col("PF", 0), v, OP.is_equal, OP.mult)
-        ts(r, col("PF", 3), col("PI", 3), 3.0, col("PF", 0), OP.mult, OP.add)
-        ts(r, col("PF", 6), col("PF", 3), 96.0, None, OP.add)
-        ts(r, ap("WW", 0, 608), ap("JR", 0, 608), col("PF", 6), None, OP.is_equal)
+        ts(r, ap("BB", 0, 144), ap("JR", 0, 144), col("PF", 2), UP, OP.is_equal, OP.mult)
+        ts(r, mat("ID"), mat("JR"), col("PF", 0), None, OP.is_equal)
+        for name, v in (("U16", UP), ("D16", DOWN)):
+            ts(r, mat(name), mat("ID"), v, None, OP.mult)
+        for name, v in (("N2", -2.0), ("P5", 5 * DOWN * UP), ("NU", -UP), ("N5", -5 * DOWN * UP), ("PU", UP), ("UD", UP * DOWN)):
+            act(r, mat(name), mat("ID"), AF.Identity, v)
+        for j in range(5):
+            ts(r, ap("WW", 128 * j, 128 * j + 96), ap("ID", 0, 96), 0.0, None, OP.mult)
+        for j in range(4):
+            ts(r, ap("WW", 128 * j + 96, 128 * j + 128), ap("ID", 32 * j, 32 * j + 32), DOWN, None, OP.mult)
         if r in WORKERS:
-            iota(r, mat("JM"), [[0, 4], [1, 32]], 0, 0)
+            behind(iota(r, mat("JM"), [[0, 4], [1, 32]], 0, 0))
             cp(r, col("PF", 1), col("PI", 1))
-            for name in ("L16", "LB", "L32"):
-                ts(r, mat(name), mat("JM"), col("PF", 1), 0.25, OP.is_equal, OP.mult)
+            ts(r, mat("LB"), mat("JM"), col("PF", 1), 0.25, OP.is_equal, OP.mult)
+            cp(r, mat("L16"), mat("LB"))
+            act(r, mat("L32"), mat("LB"))
             ts(r, col("PF", 4), col("PI", 1), 4.0, 1.0, OP.mult, OP.add)
             ts(r, col("PF", 5), col("PI", 4), 0.0625, col("PF", 4), OP.mult, OP.add)
             ts(r, ap("FF", 0, 136), ap("JR", 0, 136), col("PF", 5), 0.25, OP.is_equal, OP.mult)
 
+    tag[0] = "xr"
     for r in range(N):
         for src, stage, slot in ([("tb", "TD", 4)] if r == 0 else []) + [("x", "XD", r)]:
             moves = []
@@ -244,140 +320,183 @@ def build(cores, topo):
                     moves.append((d, ap("XL", 0, 512, lead=slot), ap(stage, 0, 512, lead=k)))
             send(r, moves)
     for k, r in enumerate(WORKERS):
+        first, last = gone(r), []
         for slot, name, src, owner in [(4, "TB", "tb", 0)] + [(t, "XR%d" % t, "x", t) for t in range(4)]:
             for q in range(4):
                 frm = ap(src, 0, W, p0=32 * k, p1=32 * k + 32) if owner == r else ap("XL", 0, 512, lead=slot)
-                dma(r, ap(name, 0, W, p0=32 * q, p1=32 * q + 32), frm, after=gates[r])
+                i = dma(r, ap(name, 0, W, p0=32 * q, p1=32 * q + 32), frm, after=first)
+                nodes[i - 1]["soft"] += [j - 1 for j in last]
+                last = [i] if q == 0 else last
 
     def blk(name, m, s):
         return ap(name, 128 * m + 64 * s, 128 * m + 64 * s + 64)
 
-    defer = PAR["defer"]
+    defer, mix = PAR["defer"], pieces(PAR["mix"])
+    nm = sum(v for p, v in mix if p == "M")
     for r in range(N):
+        tag[0] = "pre"
         turn(0)
+        once = PAR["once"][r]
         for s in range(2):
             cp(r, blk("OFF", 0, s), blk("C0", 0, s))
-        ts(r, mat("CK"), mat("C0"), float(BASE), None, OP.add)
+        ts(r, mat("CK"), mat("C0"), float(BASE), 1 / DOWN, OP.add, OP.mult)
         for s in range(2):
-            n = max(sum(PAR["dve"][r][m][s][2:]) for m in range(5))
-            if n:
-                a, b = 1024 * s + 1024 - 16 * n, 1024 * s + 1024
-                act(r, ap("SQ", a, b), ap("X", a, b), AF.Square)
-                mm(r, ap("PS%d" % s, 0, n), [(ap("BB", 15 - p, 143 - p), ap("SQ", a + p, b, 16)) for p in range(16)])
-                act(r, ap("NB", 64 * s + 64 - n, 64 * s + 64), ap("PS%d" % s, 0, n))
+            ts(r, ap("NB", 64 * s, 64 * s + 64 - nm), ap("ID", 0, 64 - nm), 0.0, -2047.0, OP.mult, OP.add)
+            a, b = 1024 * s + 1024 - 16 * nm, 1024 * s + 1024
+            act(r, ap("SQ", a, b), ap("X", a, b), AF.Square)
+            mm(r, ap("PS%d" % s, 0, nm), [(ap("BB", 15 - p, 143 - p), ap("SQ", a + p, b, 16)) for p in range(16)])
+            ts(r, ap("NB", 64 * s + 64 - nm, 64 * s + 64), ap("PS%d" % s, 0, nm), 1 / UP, -2047.0, OP.mult, OP.add)
         for m in range(5):
             turn(2 * m + 0.5)
             ts(r, ap("TF", 128 * m, 128 * m + 128), ap("TH", 128 * m, 128 * m + 128), -1.0, 2048.0, OP.mult, OP.add)
+            const(r, ap("KC", 64 * m, 64 * m + 64), 3.0 * BASE + KEY * (4 * m - 1) - 2048)
+        made = {}
         for m in range(5):
             for s in range(2):
-                o, x0, lc = 128 * m + 64 * s, 1024 * s, 0
-                tab = ap("TAB", 0, WIN if m else W)
+                tag[0], w = "m%d%d" % (m, s), 2 * m + s
+                o, x0 = 128 * m + 64 * s, 1024 * s
                 pd, p2, pw, py = "PS%d" % s, "PS%d" % (2 + s), "PS%d" % (4 + s), "PS%d" % (6 + s)
-                turn(2 * m + s - 1)
-                act(r, blk("HI", m, s), blk("CK", m, s), AF.Identity, 5.0, -4.0 * BASE - 5.0 * KEY * m - 1022.5)
-                turn(2 * m + s)
-                mine, other = PAR["dve"][r][m][s][:2], PAR["dve"][r][m][s][2:]
-                u, fill = sum(mine), [0, 0]
-                rest = 64 - u - sum(other)
-                for j, n in [(0, min(16, rest - v)) for v in range(0, rest, 16)] + [(1, n) for n in other]:
-                    if n:
-                        a, b, h = x0 + 16 * u, x0 + 16 * (u + n), int(fill[1] < fill[0])
-                        ps = ap((p2, py)[h], fill[h], fill[h] + 16 * n)
-                        fill[h] += 16 * n
-                        mm(r, ps, [(mat("N2" if j else "NID"), ap("X", a, b))], end=False)
-                        act(r, ap("GA", a, b), ind(tab, ap("OFF", o + u, o + u + n)))
-                        mm(r, ps, [(mat("ID"), ap("GA", a, b))], more=True)
-                        if j:
-                            tt(r, ap("SQ", a, b), ps, ap("GA", a, b), OP.mult)
-                        else:
-                            act(r, ap("SQ", a, b), ps, AF.Square)
-                        u += n
-                for n in [n for n in mine if n]:
-                    a, b = x0 + 16 * lc, x0 + 16 * (lc + n)
-                    tt(r, ap("DIFF", a, b), ind(tab, ap("OFF", o + lc, o + lc + n)), ap("X", a, b), OP.subtract)
-                    act(r, ap("SQ", a, b), ap("DIFF", a, b), AF.Square)
-                    lc += n
-                d, ck = ap(pd, 0, 64), blk("CK", m + 1, s)
-                mm(r, d, [(mat("P5"), blk("CK", m, s)), (mat("NID"), blk("HI", m, s))], end=False)
-                if sum(other):
-                    mm(r, ap(pd, 64 - sum(other), 64), [(mat("I32"), ap("NB", 64 * s + 64 - sum(other), 64 * s + 64))], more=True, end=False)
-                mm(r, d, [(ap("BB", 15 - p, 143 - p), ap("SQ", x0 + p, x0 + 1024, 16)) for p in range(16)], more=True)
-                zero = 1.0 - 4 * BASE - 5 * KEY * m
+                cut = -4.0 * BASE - 5.0 * KEY * m
+                turn(w - 1)
+                made["h", w] = act(r, blk("HI", m, s), blk("CK", m, s), AF.Identity, 5 * DOWN, cut - 1022.5)
+                turn(w)
+                u = 0
+                for p, n in mix:
+                    a, b = x0 + 16 * u, x0 + 16 * (u + n)
+                    src = ind(ap("TAB", 0, WIN if m else W), ap("OFF", o + u, o + u + n))
+                    if p == "V":
+                        made["vw"[u > 0], w] = tt(r, ap("DIFF", a, b), src, ap("X", a, b), OP.subtract)
+                        made["qr"[u > 0], w] = act(r, ap("SQ", a, b), ap("DIFF", a, b), AF.Square)
+                    else:
+                        ps = ap(p2, 0, 16 * n)
+                        mm(r, ps, [(mat("N2"), ap("X", a, b))], end=False)
+                        made["g", w] = act(r, ap("GA", a, b), src)
+                        made["a", w] = mm(r, ps, [(mat("ID"), ap("GA", a, b))], more=True)
+                        made["m", w] = tt(r, ap("SQ", a, b), ps, ap("GA", a, b), OP.mult)
+                    u += n
+                jb = lambda name, a=0, b=256: ap(name, 256 * s + a, 256 * s + b)
+                d, z, ck = ap(pd, 0, 64), ap(py, 0, 64), blk("CK", m + 1, s) if m < 4 else jb("C4", 0, 64)
+                made["p", w] = mm(r, d, [(mat("U16"), blk("NB", 0, s)), (mat("P5"), blk("CK", m, s)), (mat("NU"), blk("HI", m, s))], end=False)
+                made["s", w] = mm(r, d, [(ap("BB", 15 - p, 143 - p), ap("SQ", x0 + p, x0 + 1024, 16)) for p in range(16)], more=True)
+                zero = cut + 2048.0
                 if m < 4:
-                    ts(r, blk("OFF", m + 1, s), d, zero, None, OP.add)
-                turn(2 * m + s + (defer[0] if m < 4 else 0))
-                zero += BASE + KEY * (m + 1)
-                act(r, ck, d, AF.Identity, 1.0, zero)
-                mm(r, d, [(mat("N5"), blk("CK", m, s)), (mat("ID"), blk("HI", m, s)), (mat("I16"), blk("TF", m, s)), (mat("I32"), ck)])
-                act(r, ap(pw, 0, 64), d, AF.Identity, BIG, -(2047.5 + zero) * BIG)
-                turn(2 * m + s + (defer[1] if m < 4 else defer[2 + (r > 1)]))
-                ws = blk("WS", m // 2, s)
-                wp = ap(pw, 64, 128) if m < 4 else ap(pw, 320, 384)
-                tt(r, ws if m in (0, 2) else wp, ap(pw, 0, 64), blk("CK", m, s), OP.max)
-                lt = lambda j, n=1: ap("LT", 256 * s + 64 * j, 256 * s + 64 * (j + n))
-                if m == 1:
-                    tt(r, ap("AA", 128 * s, 128 * s + 64), wp, ws, OP.min)
-                    tt(r, ap("AA", 128 * s + 64, 128 * s + 128), wp, ws, OP.max)
-                if m == 3:
-                    aa = ap("AA", 128 * s, 128 * s + 128)
-                    tt(r, ap(pw, 128, 192), wp, ws, OP.min)
-                    tt(r, ap(pw, 192, 256), wp, ws, OP.max)
-                    tt(r, ap(pw, 256, 384), ap(pw, 128, 256), aa, OP.min)
-                    tt(r, lt(2, 2), ap(pw, 128, 256), aa, OP.max)
-                    tt(r, ap(pw, 384, 448), ap(pw, 320, 384), lt(2), OP.min)
-                    tt(r, ap(pw, 448, 512), ap(pw, 320, 384), lt(2), OP.max)
+                    made["o", w + 2] = ts(r, blk("OFF", m + 1, s), d, 1 / UP, zero, OP.mult, OP.add)
+                turn(w + defer[0])
+                made["c", w + 2] = act(r, ck, d, AF.Identity, 1 / (UP * DOWN), (zero + BASE + KEY * (m + 1)) / DOWN)
+                for j in range(1, 4 * (m == 4)):
+                    act(r, jb("C4", 64 * j, 64 * j + 64), d, AF.Identity, 1 / (UP * DOWN), (zero + BASE + KEY * (m + 1)) / DOWN)
+                made["z", w + 2] = mm(r, z, [(mat("N5"), blk("CK", m, s)), (mat("PU"), blk("HI", m, s)), (mat("PU"), ap("KC", 64 * m, 64 * m + 64)),
+                                             (mat("U16"), blk("TF", m, s)), (mat("UD"), ck)])
+                turn(w + (defer[1] if m < 4 else defer[2]))
+                ws, wp = blk("WS", m // 2, s), ap(pw, 64, 128)
                 if m == 4:
-                    for j, a in enumerate((256, 384, 448)):
-                        tt(r, lt(j), ap(pw, a, a + 64), ck, OP.min)
-                    tt(r, ap(pw, 0, 64), wp, ck, OP.min)
+                    tag[0] = "sel%d" % s
+                lt = lambda j, n=1: jb("LT", 64 * j, 64 * (j + n))
+                cuts = [(0, 256, ap(p2, 256, 512))] if once else [(0, 128, ap(p2, 256, 384)), (128, 256, ap(pw, 0, 128))]
+                if m == 4:
+                    for a, b, keyed in cuts:
+                        tt(r, keyed, ap(pw, 192 + a, 192 + b), jb("C4", a, b), OP.min)
+                tt(r, ws if m in (0, 2) else lt(0) if m == 4 else wp, z, blk("CK", m, s), OP.max)
+                aa = lambda a, b: ap("AA", 128 * s + a, 128 * s + b)
+                if m == 1:
+                    tt(r, aa(0, 64), wp, ws, OP.min)
+                    tt(r, aa(64, 128), wp, ws, OP.max)
+                if m == 3:
+                    tt(r, ap(pw, 384, 448), wp, ws, OP.min)
+                    tt(r, ap(pw, 448, 512), wp, ws, OP.max)
+                    tt(r, ap(pw, 192, 320), ap(pw, 384, 512), aa(0, 128), OP.min)
+                    tt(r, ws, ap(pw, 384, 448), aa(0, 64), OP.max)
+                    tt(r, ap(pw, 384, 448), ap(pw, 448, 512), aa(64, 128), OP.max)
+                    tt(r, ap(pw, 320, 384), ap(pw, 256, 320), ws, OP.max)
+                    tt(r, ap(pw, 256, 320), ap(pw, 256, 320), ws, OP.min)
+                if m == 4:
                     for j in range(3):
-                        tt(r, ap(pw, 64 * j + 64, 64 * j + 128), ap(pw, 0, 64), lt(j), OP.max)
-                    jb = lambda name, a=0, b=256: ap(name, 256 * s + a, 256 * s + b)
-                    keyed = ap(pw, 256, 512)
-                    tt(r, keyed, ap(pw, 0, 256), lt(0, 4), OP.min)
-                    act(r, jb("JK"), keyed, AF.Identity, 1.0, -1023.5)
-                    tt(r, jb("JH"), keyed, jb("JK"), OP.subtract)
+                        tt(r, lt(j + 1), ap(pw, 192 + 64 * j, 256 + 64 * j), lt(0), OP.max)
+                    for a, b, keyed in cuts:
+                        tt(r, keyed, keyed, lt(a // 64, (b - a) // 64), OP.min)
+                    for a, b, keyed in cuts:
+                        act(r, jb("JK", a, b), keyed, AF.Identity, 1.0, -1023.5 / DOWN)
+                        tt(r, jb("JH", a, b), keyed, jb("JK", a, b), OP.subtract)
                     perm = lambda k, q: ap("WW", 128 * k + 96 - 32 * q, 128 * k + 224 - 32 * q)
-                    for k in range(4):
-                        if r < N - 1:
-                            mm(r, ap(py, 64 * k, 64 * k + 64), [(perm(k, q), jb("JH", 64 * q, 64 * q + 64)) for q in range(4)])
-                        else:
-                            for u in range(2):
-                                at = lambda q: 64 * (2 * (q // 2) + u) + 32 * (q % 2)
-                                mm(r, ap(py, 64 * k + 32 * u, 64 * k + 32 * u + 32), [(perm(k, q), jb("JH", at(q), at(q) + 32)) for q in range(4)])
-                    cp(r, jb("JS"), ap(py, 0, 256))
-                    send(r, [(d2, blk("OFT", r, s), jb("JS", 64 * k, 64 * k + 64)) for k, d2 in enumerate(WORKERS) if d2 != r])
-                    turn(30)
-                    mm(r, ap(pw, 0, 256), [(mat("I16"), jb("JH"))])
-                    for q in range(4):
-                        act(r, blk("YJ", q, s), ap(pw, 64 * q, 64 * q + 64))
-        turn(defer[4])
-        dma(r, ap("yj", 0, 512), ap("YJ", 0, 512))
+                    for part in ([range(4)] if once else PAR["parts"][s]):
+                        moves = []
+                        for k in part:
+                            bank, c = ("PS6", 128 * k + 64 * s) if once else (py if 3 in part else pd, 64 * k)
+                            if r < N - 1:
+                                mm(r, ap(bank, c, c + 64), [(perm(k, q), jb("JH", 64 * q, 64 * q + 64)) for q in range(4)])
+                            else:
+                                for u in range(2):
+                                    at = lambda q: 64 * (2 * (q // 2) + u) + 32 * (q % 2)
+                                    mm(r, ap(bank, c + 32 * u, c + 32 * u + 32), [(perm(k, q), jb("JH", at(q), at(q) + 32)) for q in range(4)])
+                            moves += [(WORKERS[k], blk("OFT", r, s), jb("JS", 64 * k, 64 * k + 64))] if WORKERS[k] != r else []
+                        if not once:
+                            far = [k for k in part if WORKERS[k] != r]
+                            cp(r, jb("JS", 64 * far[0], 64 * far[-1] + 64), ap(bank, 64 * far[0], 64 * far[-1] + 64))
+                            send(r, moves)
+                            for k in set(part) - set(far):
+                                cp(r, blk("OFT", r, s), ap(bank, 64 * k, 64 * k + 64))
+                    if once and s == 1:
+                        cp(r, ap("JS", 0, 512), ap("PS6", 0, 512))
+                        send(r, [(d2, ap("OFT", 128 * r, 128 * r + 128), ap("JS", 128 * k, 128 * k + 128)) for k, d2 in enumerate(WORKERS) if d2 != r])
+        mine = [i for i, v in enumerate(nodes) if v["r"] == r and v["eng"] == "V"]
+        for i in mine:
+            if nodes[i]["tag"] == "sel1":
+                nodes[i]["soft"] += [j for j in mine if nodes[j]["tag"] == "sel0"][:PAR["first"][r]]
+        for lst in PAR["beat"]:
+            last = []
+            for w in range(12):
+                for ch, back in pieces(lst):
+                    if (ch, w + 1 - back) in made:
+                        nodes[made[ch, w + 1 - back]]["soft"] += last
+                        last = [made[ch, w + 1 - back]]
+
+    def parents_out(r):
+        tag[0] = "yj"
+        for s in range(2):
+            for q in range(4):
+                mm(r, blk("PS7", q, s), [(mat("D16"), ap("JH", 256 * s + 64 * q, 256 * s + 64 * q + 64))])
+        act(r, ap("YJ", 0, 512), ap("PS7", 0, 512))
+        dma(r, ap("yj", 0, 512), ap("YJ", 0, 512), after=gone(r))
 
     def lists(r, t, a, b):
-        if t == r:
-            base = 256 * (a // 64) + 64 * WORKERS.index(r) + a % 64
+        if t == r and PAR["once"][r]:
+            base = 128 * WORKERS.index(r) + a
             return ap("JS", base, base + b - a)
         return ap("OFT", 128 * t + a, 128 * t + b)
 
     def piece(k, b):
         return ap("ytau", 1024 * b, 1024 * b + 1024, p0=32 * k, p1=32 * k + 32)
 
+    staged, ready, stores = {}, {}, []
+
+    def hand(r, names):
+        i = send(r, [ready[(r, v)] for v in names])
+        for v in names:
+            d, out, a = ready[(r, v)]
+            stores.append((d, len(nodes)))
+            dma(d, piece(out[1] // 2, out[1] % 2), out, q="A" if d == N - 1 and out[1] // 2 % 2 else "S")
+        return i
+
+    turn(defer[3])
+    for r in range(N):
+        parents_out(r)
     for t in range(4):
         for k, r in enumerate(WORKERS):
+            tag[0] = "t%d" % t
             win = ap("TB" if t == 0 else "T%d" % (t - 1), 0, W)
-            plan, b = PAR["steps"][k][t], 0
-            for c in range(len(plan) // 2):
-                how, n = plan[2 * c], 128 * int(plan[2 * c + 1])
-                a, b = b, b + n
+            b, made = 0, {}
+            plan = PAR["steps"][t].split()
+            for c, (how, n) in enumerate(pieces(plan[0])):
+                a, b = b, b + 64 * n
+                first = len(nodes)
                 src = ind(win, lists(r, t, a // 16, b // 16))
-                ps = ap("PS%d" % (c % 4 if t == 0 else c % 8), 0, n)
+                ps = ap("PS" + (PAR["banks"][c] if t == 0 else str(c % 8)), 0, b - a)
                 xr, out = ap("XR%d" % t, a, b), ap("T%d" % t, a, b)
-                if how in "DE":
+                if how == "D":
                     gb = ap("G16" if t < 2 else "G32", a, b)
                     tt(r, gb, src, xr, OP.add)
                     pairs = [(mat("L16" if t < 2 else "L32"), gb)]
-                elif how in "AY":
+                elif how == "A":
                     gb = ap("GH" if t == 0 else "G32", a, b)
                     act(r, gb, src)
                     pairs = [(mat("LB" if t == 0 else "L32"), gb)]
@@ -385,92 +504,158 @@ def build(cores, topo):
                     act(r, ap("GH", a, b), src)
                     tt(r, ap("GL", a, b), src, ap("GH", a, b), OP.subtract)
                     pairs = [(mat("LB"), ap("GH", a, b)), (mat("LB"), ap("GL", a, b))]
-                mm(r, ps, ([(mat("LB"), xr)] if how in "YX" else []) + pairs)
-                if how in "AS":
+                mm(r, ps, pairs)
+                if how == "D":
+                    act(r, out, ps)
+                else:
                     tt(r, out, ps, xr, OP.add)
-                else:
-                    (cp if how == "E" else act)(r, out, ps)
+                for i, v in zip(range(first, len(nodes)), "hlpe" if how == "S" else "gpe"):
+                    made[v + str(c)] = i
+            follow(made, plan[1:])
+            if t == r == 0:
+                for i in made.values():
+                    nodes[i]["soft"] += [j for j, v in enumerate(nodes) if v["r"] == r and v["tag"][:3] == "sel" and v["eng"] == nodes[i]["eng"]]
+            tag[0] = "o%d" % t
             for b in range(2):
-                rows = ap("T%d" % t, 1024 * b, 1024 * b + 1024, p1=32)
-                if r == t:
-                    dma(r, piece(k, b), rows)
-                else:
-                    dma(r, ap("OD", 0, 256, lead=2 * t + b), rows)
-                    send(r, [(t, ap("LD", 0, 256, lead=2 * k + b), ap("OD", 0, 256, lead=2 * t + b))])
-                    dma(t, piece(k, b), ap("LD", 0, 256, lead=2 * k + b))
-    t, n = N - 1, PAR["fin"]
+                staged[(r, t, b)] = len(nodes)
+                dma(r, piece(k, b) if r == t else ap("OD", 0, 256, lead=2 * t + b), ap("T%d" % t, 1024 * b, 1024 * b + 1024, p1=32))
+                ready[(r, "ab"[b])] = (t, ap("LD", 0, 256, lead=2 * k + b), ap("OD", 0, 256, lead=2 * t + b))
+            if r != t and t < 3:
+                hand(r, "ab")
+        for (d, i) in stores:
+            if (d, t, 1) in staged and d + 1 == t:
+                nodes[i]["soft"] += [staged[(d, t, 0)], staged[(d, t, 1)]]
+    t, made = N - 1, [{} for r in range(N)]
     for b in range(2):
         for k, r in enumerate(WORKERS):
-            win = ap("T3", 0, W)
-            for c in range(0, 256, n):
-                pairs = [(mat("ID"), ap("XC", 256 * b + c, 256 * b + c + n))]
+            tag[0] = "t4"
+            win, c = ap("T3", 0, W), 0
+            for j, (how, n) in enumerate(pieces(PAR["fin"][b])):
+                xc, ps = ap("XC", 256 * b + c, 256 * b + c + n), ap("PS%d" % (4 * b + j), 0, n)
+                pairs = [(mat("ID"), xc)] if how == "P" else []
+                num = len(pieces(PAR["fin"][0])) * b + j
                 for jj in range(2):
                     a, lc = 512 * b + 256 * jj + c, 64 * b + 16 * jj + c // 16
-                    act(r, ap("G32", a, a + n), ind(win, lists(r, t, lc, lc + n // 16)))
-                    tt(r, ap("G32", 1024 + a, 1024 + a + n), ind(win, lists(r, t, lc + 32, lc + 32 + n // 16)), ap("G32", a, a + n), OP.add)
-                    pairs.append((ap("FF", 1 - jj, 129 - jj), ap("G32", 1024 + a, 1024 + a + n)))
-                ps = ap("PS%d" % ((256 * b + c) // n % 8), 0, n)
-                mm(r, ps, pairs)
-                (cp if b == 1 and c + n == 256 else act)(r, ap("FIN", 256 * b + c, 256 * b + c + n), ps)
-            fin = ap("FIN", 256 * b, 256 * b + 256)
+                    ga, gv, at = ap("G32", a, a + n), ap("G32", 1024 + a, 1024 + a + n), str(2 * num + jj)
+                    made[r]["a" + at] = act(r, ga, ind(win, lists(r, t, lc, lc + n // 16)))
+                    made[r]["v" + at] = tt(r, gv, ind(win, lists(r, t, lc + 32, lc + 32 + n // 16)), ga, OP.add)
+                    made[r]["p" + at] = mm(r, ps, pairs + [(ap("FF", 1 - jj, 129 - jj), gv)], more=jj == 1, end=jj == 1)
+                    pairs = []
+                fin = ap("FIN", 256 * b + c, 256 * b + c + n)
+                made[r]["e" + str(num)] = act(r, fin, ps) if how == "P" else tt(r, fin, ps, xc, OP.add)
+                c += n
+            tag[0] = "o4"
+            ready[(r, "fg"[b])] = (t, ap("LD", 0, 256, lead=2 * k + b), ap("FIN", 256 * b, 256 * b + 256))
             if r == t:
-                dma(r, piece(k, b), fin)
-            else:
-                send(r, [(t, ap("LD", 0, 256, lead=2 * k + b), fin)])
-                dma(t, piece(k, b), ap("LD", 0, 256, lead=2 * k + b), q="S" if k % 2 == 0 else "A")
+                dma(r, piece(k, b), ap("FIN", 256 * b, 256 * b + 256))
+    for r in WORKERS:
+        last = []
+        for names in PAR["last"][r].split():
+            i = hand(r, names)
+            nodes[i]["soft"], last = last, [i]
+        follow(made[r], PAR["fin"][2:])
     return nodes
 
 
-def schedule(nodes):
-    HOP = 60.0
-    n = len(nodes)
-    users = [[] for _ in range(n)]
-    for i, v in enumerate(nodes):
-        for d in v["deps"]:
-            users[d].append(i)
-    way = [0.0] * n
-    for i in range(n - 1, -1, -1):
-        way[i] = nodes[i]["busy"] + nodes[i]["lat"] + max([way[u] + HOP for u in users[i]] + [0.0])
-    left = [len(v["deps"]) for v in nodes]
-    ready_at, done, start = [0.0] * n, [0.0] * n, [0.0] * n
-    free, ready, order = {}, {}, {}
+def rising(links, back, key):
+    key, left = list(key), [len(b) for b in links[back]]
+    todo = [i for i, c in enumerate(left) if not c]
+    while todo:
+        i = todo.pop()
+        for u, gap in links[1 - back][i]:
+            key[u] = max(key[u], key[i] + 1e-3)
+            left[u] -= 1
+            if not left[u]:
+                todo.append(u)
+    return sorted(range(len(key)), key=lambda i: (key[i], i))
 
-    def release(i):
+
+def place(nodes, links, key, back):
+    end, used = [0.0] * len(nodes), {}
+    for i in rising(links, back, key):
         v = nodes[i]
-        if v["eng"] is None:
-            finish(i, ready_at[i])
-        else:
-            ready.setdefault((v["r"], v["eng"]), []).append(i)
+        t = max([v["lat"] if back else 0.0] + [end[d] + gap for d, gap in links[back][i]])
+        if v["eng"]:
+            lst = used.setdefault((v["r"], v["eng"]), [])
+            j = len(lst)
+            while j and lst[j - 1][1] > t:
+                j -= 1
+            while j < len(lst) and lst[j][0] < t + v["busy"]:
+                t = max(t, lst[j][1])
+                j += 1
+            lst.insert(j, (t, t + v["busy"]))
+        end[i] = t + v["busy"]
+    return end
+
+
+def greedy(nodes, links):
+    n = len(nodes)
+    way = [0.0] * n
+    for i in rising(links, 1, [0.0] * n):
+        way[i] = nodes[i]["busy"] + max([nodes[i]["lat"]] + [way[u] + gap for u, gap in links[1][i]])
+    left, at, end = [len(b) for b in links[0]], [0.0] * n, [0.0] * n
+    free, ready = {}, {}
 
     def finish(i, t0):
-        start[i] = t0
-        done[i] = t0 + nodes[i]["busy"] + nodes[i]["lat"]
-        for u in users[i]:
-            ready_at[u] = max(ready_at[u], done[i] + (HOP if nodes[u]["eng"] else 0.0))
+        end[i] = t0 + nodes[i]["busy"]
+        for u, gap in links[1][i]:
+            at[u] = max(at[u], end[i] + gap)
             left[u] -= 1
             if left[u] == 0:
                 release(u)
 
-    for i in range(n):
-        if not nodes[i]["deps"]:
-            release(i)
+    def release(i):
+        if nodes[i]["eng"] is None:
+            finish(i, at[i])
+        else:
+            ready.setdefault((nodes[i]["r"], nodes[i]["eng"]), []).append(i)
+
+    for i in [i for i in range(n) if not left[i]]:
+        release(i)
     while True:
-        best = None
-        for q, lst in ready.items():
-            if lst:
-                t0 = max(free.get(q, 0.0), min(ready_at[i] for i in lst))
-                if best is None or t0 < best[0]:
-                    best = (t0, q)
-        if best is None:
-            break
-        t0, q = best
-        i = max((i for i in ready[q] if ready_at[i] <= t0 + PAR["window"]), key=lambda i: (way[i] + nodes[i]["lead"], -i))
+        soon = [(max(free.get(q, 0.0), min(at[i] for i in lst)), q) for q, lst in ready.items() if lst]
+        if not soon:
+            return end
+        t0, q = min(soon)
+        i = max((i for i in ready[q] if at[i] <= t0), key=lambda i: (way[i] + nodes[i]["lead"], -i))
         ready[q].remove(i)
-        t0 = max(t0, ready_at[i])
         free[q] = t0 + nodes[i]["busy"]
-        order.setdefault(q, []).append(i)
         finish(i, t0)
-    return order, start, done
+
+
+def hop(a, b):
+    if a["eng"] == b["eng"] == "P":
+        return 0.0
+    return a["lat"] + ((COST["HS"] if a["eng"] == b["eng"] else COST["HOP"]) if b["emit"] else 0.0)
+
+
+def schedule(nodes):
+    n = len(nodes)
+    soft = [list(v["soft"]) for v in nodes]
+    for q, code in ORDER.items():
+        rest, skip, last = [i for i, v in enumerate(nodes) if (v["r"], v["eng"]) == q], 0, []
+        for ch in code:
+            skip += LETTERS.index(ch)
+            if ch != LETTERS[-1]:
+                i, skip = rest.pop(skip), 0
+                soft[i], last = last, [i]
+    links = ([[] for _ in range(n)], [[] for _ in range(n)])
+    for i, v in enumerate(nodes):
+        for d, gap in [(d, hop(nodes[d], v)) for d in sorted(v["deps"])] + [(d, 0.0) for d in soft[i]]:
+            links[0][i].append((d, gap))
+            links[1][d].append((i, gap))
+    end, best = greedy(nodes, links), None
+    for _ in range(5):
+        span = max(e + v["lat"] for e, v in zip(end, nodes)) + 0.2 * sum(end) / n
+        if best is None or span < best[0]:
+            best = (span, end)
+        end = place(nodes, links, [-e for e in place(nodes, links, [-e for e in end], 1)], 0)
+    start = [e - v["busy"] for e, v in zip(best[1], nodes)]
+    order = {}
+    for i in sorted(range(n), key=lambda i: (start[i], i)):
+        if nodes[i]["eng"]:
+            order.setdefault((nodes[i]["r"], nodes[i]["eng"]), []).append(i)
+    return order, start, [e + v["lat"] for e, v in zip(best[1], nodes)]
 
 
 def waits(nodes, order, start):
@@ -487,7 +672,7 @@ def waits(nodes, order, start):
     known, clock, need = {}, {}, {}
     for i in sorted(range(len(nodes)), key=lambda i: (start[i], i)):
         v = nodes[i]
-        if v["eng"] is None:
+        if v["emit"] is None:
             clock[i] = {}
             continue
         k = known.setdefault((v["r"], v["eng"]), {})
@@ -520,7 +705,7 @@ def rank_program(g, core, T, topo):
     for i, v in enumerate(nodes):
         if v["r"] == r and mark[i][0]:
             top[mark[i][0]] = max(top.get(mark[i][0], 0), mark[i][1])
-    mine = [i for (r2, eng), lst in order.items() if r2 == r for i in lst]
+    mine = [i for (r2, eng), lst in order.items() if r2 == r for i in lst if nodes[i]["emit"]]
     for i in sorted(mine, key=lambda i: (start[i], i)):
         v = nodes[i]
         for name, c in need[i].items():
@@ -528,7 +713,8 @@ def rank_program(g, core, T, topo):
             got[name] = max(got.get(name, 0), c)
         ins = v["emit"](g, T)
         if ins is not None:
-            ins.then_inc(T.sem[mark[i][0]], 1 if v["sem"] is None else v["sem"][1])
+            name, c = v.get("inc", (mark[i][0], 1))
+            ins.then_inc(T.sem[name], c)
     for name, c in top.items():
         if got.get(name, 0) < c:
             g.wait_ge(T.sem[name], c)

@@ -4,56 +4,45 @@ from concourse.mybir import ActivationFunctionType as AF
 
 N = 5
 W = 2048
-WORKERS = [0, 2, 3, 4]
+WORKERS = [1, 2, 3, 4]
 WIN = 5648
 KEY = 8192
 BASE = 129 * W
 DOWN = 128.0
 UP = 4096.0
 
-COST = {"CY": 0.92, "PE": 0.46, "G": 1.56, "LAT": 0, "HOP": 200, "HS": 20, "DMA": 1820, "FAR": 850, "CALL": 130, "ROW": 12,
-        "FIRST": 600, "RATE": 1000, "RR": 780, "DD": 1, "VF": 33, "AF": 36, "MF": 5, "SI": 76}
-STEP2 = "A4S7D1S5A3D6D6 g6g5l1l3g2e4e1e3e0 g4h1h3g0e6e5e2 p4p6p5p1p3p0p2"
 PAR = {
-    "load": ["02 28 xb th"] + ["02 28 th"] * 4,
-    "mix": "V20V20M24",
-    "beat": ["o1m2v1w1", "r2g1c1h1q1", "s2a1z1p1"],
-    "steps": ["D8A8D4A4D4A4", "A2D6A4D4D6A4D4A2", STEP2, STEP2], "banks": "012301",
-    "fin": ["P128P128", "p128p128", "v0v1v2v3v4v5v6v7e2e3", "a0a1a2a3a4a5a6a7e0e1", "p0p1p2p3p4p5p6p7"],
-    "defer": [0, 2.5, 1.5, 20], "once": [0, 0, 1, 1, 1], "first": [10, 8, 0, 0, 0],
-    "parts": [[[0, 1, 2, 3]], [[2, 3], [0, 1]]],
-    "last": ["f ab g", "", "f ab g", "f g", "ab"],
+    "load": ["02 xb 28 th"] + ["02 28 th"] * 3 + ["08 th"],
+    "repeats": ["v1 h2 s1 s2", "s1 s2", "s2", "v1 s1 s2", ""],
+    "mix": ["V20V20M24"] * 3 + ["V22V20M22"] * 2,
+    "loose": [0, 1],
+    "ahead": [[0, 3], [0, 0]],
+    "chooser": [0, 1, 2, 0, 0],
+    "choose": "q0052 q0163 q1052 q1163 l267 l304 l417 s052 s163",
+    "steps": ["D8A8D4D5A7", "A3D6A4D3D7A2D4A3", "A1S5S8T3D6D6B2A1", "A1S5S8T3D6D6B2A1"],
+    "banks": ["", "014701", "012345", "012345", "012345"],
+    "fin": ["p128P128", "p128", "p128"], "solo": [0],
+    "last": ["", "f a b g h", "f a b g h", "f g h", "a b"],
 }
 LETTERS = "0123456789abcdefghijklmnopqrstuvwxyzABCDEFGHIJKLMNOPQRSTUVWXYZ+"
-ORDER = {
-    (0, "V"): "wxyzA014232lm33333333aba302102229923268867992256499584bb262829227562772234dd23bkk2aiv2t22r7225342297998777222233662564444233201000000110122311008713231108713231100000001100",
-    (0, "A"): "0000000114111522261222612226122261222612226132261222b19135241343111113642220020340000412021041202100011222200",
-    (0, "P"): "26000001131204112013120411201312240125011201716004442210001028304134100200211210004541200454120000000000",
-    (3, "V"): "wxyzA014232lm02a22222aba2221022555550200000022013312055140773607005340650012cb2aj0i08gon00010i00008098000100102012211001212110132321008713231108713231100000001100",
-    (3, "A"): "00000001103000411150111501115011150111501215012104210085632020211100234111351500100412021041202100011222200",
-    (3, "P"): "26000001131204112013120411204112013120411290116050442088893376001030000010213200104541200454120000000000",
-    (4, "V"): "wxyzA014232lm02a2928bcb42322210555550200000022013312055140773607005346050012cb2ak0i90g0mm101j034191108054033100243200001212110132321008713231108713231100000001100",
-    (4, "A"): "0000000000300041115011150111501115011150211503115012190504031023110023411135610010041202104120210001122220000",
-    (4, "P"): "26000001131204112013120411201312013125201201b1aa008824e012c01c00451125745144510010213200104541200454120000000000",
-}
-for _e in "VAP":
-    ORDER[(2, _e)] = ORDER[(3, _e)]
+ORDER = {"0A":"0112300b6112112201502115031150211502161031104316101215010101010000101111","0S":"100104434110043433211","0G":"440010000001","1A":"003001511010425102150211501115021150211502115021104110520210001001301006122000721123021072114201101001111","1S":"0002008888cccc88884444000011215443312121","1G":"544001002000021","2A":"0000000000002004111501115021150211503115021104211041105201100024121310341100726112301072150031101001111","2S":"000000cccc888888884444000011000327623311","2G":"43300000002","3A":"01010000121502500210411150311502115031150111043110411600121001300001532000726100121072112430101101111","3S":"000000gggg88888888444400001111110105412","3G":"544001","4A":"00003201110042003110411104111501115021150211501210411052011001301001522000721514201072214201104113011","4S":"00622501230110gggg888888884444000011112121000033001","0V":"32211112abcfd733211077a068075177505a958cc80acca2eacc1181fe271j1a20e1d70d1b0101a7a608760100013332021000020110002422aab081761141304402121655252224313321","3V":"1255331hijkl155111111113541331211141300133125420244236042355023604202ee2g1c0c2b00103211100001100412310106631321006631321000022011201","1V":"05514k0k12j92220f0030355461220101040220331266204884791805688626cc304107dd700dab0491202010602220164503302401432010412300106631321006631321000020111011","2V":"01423202fghij03300000004544400011002201331244202442025420244012440612dd20db0b0a100213110322100200002432204420310006631321006631321100020111011","4G":"0100000001","4V":"0123013ghijk34300410000445540101113300133124401244012442024401254202ee01ee0b20a200113210000210041231200663132110663132100004224012","0P":"77220000411252236122302233304423a30330203120133111000030100100e05abaccb111005011","1P":"2106130203120411220312501125011250112041132500430010002000100000110035000103664421100736442110001","2P":"2001020141120131201312041125011250112013173200330220103303212210201110103664421100736442111001","3P":"260014024012013120131250112520122031204110114420011100000100310021036644211007364421100011","4P":"2600100141120131220312501120131204112501170110331010000011003103010366442111073644211000311"}
 
 SCRATCH = {"XD": ("dram", [4, 128, 512], "bfloat16"), "TD": ("dram", [4, 128, 512], "bfloat16"), "XL": ("dram", [5, 128, 512], "bfloat16"),
-           "OD": ("dram", [8, 128, 256], "float32"), "LD": ("dram", [8, 128, 256], "float32")}
+           "OD": ("dram", [8, 128, 256], "float32"), "LD": ("dram", [8, 128, 256], "float32"),
+           "L128": ("dram", [16, 128, 128], "float32"), "L256": ("dram", [16, 128, 256], "float32")}
 for _d, _l in (("bfloat16", "X:2048 TAB:5648 ID:128 N2:128 PU:128 NU:128 BB:144 LB:128 DIFF:2048 SQ:2048 GA:2048 HI:640 KC:320 JK:512 "
                             "TB:2048 XC:512 GH:2048 GL:2048 XR0:2048 XR1:2048 XR2:2048 XR3:2048"),
-               ("float32", "JR:144 JM:128 PF:8 L32:128 FF:136 P5:128 N5:128 UD:128 CK:640 C4:512 WS:256 AA:256 LT:512 YJ:512 FIN:512 "
+               ("float32", "JR:144 JM:128 PF:8 L32:128 FF:136 P5:128 N5:128 UD:128 CK:640 I32:128 AA:384 JL:512 KL0:512 KL1:512 "
+                           "KK0:1152 KK1:1152 KK2:1152 KK3:1152 KK4:1152 YJ0:512 YJ1:512 YJ2:512 YJ3:512 YJ4:512 FIN:512 "
                            "G32:2048 T0:2048 T1:2048 T2:2048 T3:2048"),
-               ("float16", "TF:640 U16:128 D16:128 NB:128 WW:608 L16:128 JH:512 G16:2048"),
-               ("int32", "C0:128 TH:640 PI:8"), ("uint16", "OFF:640 JS:512 OFT:640")):
+               ("float16", "TF:640 U16:128 D16:128 NB:128 L16:128 JH0:512 JH1:512 JH2:512 JH3:512 JH4:512 G16:2048"),
+               ("int32", "C0:128 TH:640 PI:8"), ("uint16", "OFF:640 JS:2560 OFT:640")):
     for _s in _l.split():
         SCRATCH[_s.split(":")[0]] = ("sbuf", [128, int(_s.split(":")[1])], _d)
 for _b in range(8):
     SCRATCH["PS%d" % _b] = ("psum", [128, 512], "float32")
-SEMAPHORES = ["cV", "cA", "cP", "cG"] + ["s%d" % _i for _i in range(120)]
-SIZE = {"bfloat16": 2, "float16": 2, "uint16": 2, "float32": 4, "int32": 4}
-IO = {"x": "bfloat16", "xb": "bfloat16", "tb": "bfloat16", "c0": "int32", "th": "int32", "yj": "float32", "ytau": "float32"}
+SEMAPHORES = ["cV", "cA", "cP", "cG"] + ["s%d" % _i for _i in range(140)]
+IO = ("x", "xb", "tb", "c0", "th", "yj", "ytau")
 
 
 def ap(name, c0, c1, step=1, p0=0, p1=128, lead=None):
@@ -79,22 +68,6 @@ def real(T, a):
     return T[name][p0:p1, c0:c1]
 
 
-def width(a):
-    return (a[5] - a[4] + a[6] - 1) // a[6]
-
-
-def esize(a):
-    return SIZE[IO[a[0]] if a[0] in IO else SCRATCH[a[0]][2]]
-
-
-def in_psum(a):
-    return a[0].startswith("PS")
-
-
-def in_sbuf(a):
-    return a[0] in SCRATCH and SCRATCH[a[0]][0] == "sbuf"
-
-
 def pieces(s):
     out = []
     for ch in s:
@@ -106,14 +79,13 @@ def pieces(s):
 
 
 def build(cores, topo):
-    CY, PE, G, LAT = COST["CY"], COST["PE"], COST["G"], COST["LAT"]
-    nodes, seen, banks, pool, lead, tag, sent = [], {}, {}, [0] * N, [0.0], ["pre"], set()
+    nodes, seen, banks, pool = [], {}, {}, [0] * N
 
     def new_sem(r):
         pool[r] += 1
         return "s%d" % (pool[r] - 1)
 
-    def add(r, eng, emit, reads, writes, busy, lat=0.0, after=(), sem=None):
+    def add(r, eng, emit, reads, writes, after=(), sem=None):
         i, deps = len(nodes), set(after)
         flat = []
         for a in reads:
@@ -125,7 +97,7 @@ def build(cores, topo):
             for (b, bw, j) in seen.setdefault((r, a[0], a[1]), []):
                 if (wr or bw) and a[2] < b[3] and b[2] < a[3] and a[4] < b[5] and b[4] < a[5]:
                     deps.add(j)
-        for name in set(a[0] for a, wr in flat if in_psum(a)):
+        for name in set(a[0] for a, wr in flat if a[0].startswith("PS")):
             st = banks.setdefault((r, name), [eng, [], []])
             if st[0] != eng:
                 st[0], st[1], st[2] = eng, [], st[1]
@@ -135,68 +107,50 @@ def build(cores, topo):
             if a[0] not in IO:
                 seen[(r, a[0], a[1])].append((a, wr, i))
         deps.discard(i)
-        name = "%s%d" % (writes[0][0], writes[0][4]) if writes else "send"
-        nodes.append({"lead": lead[0], "r": r, "eng": eng, "emit": emit, "deps": deps, "busy": busy, "lat": lat, "sem": sem,
-                      "tag": tag[0], "name": name, "soft": []})
+        nodes.append({"r": r, "eng": eng, "emit": emit, "deps": deps, "sem": sem, "left": eng is None and not writes})
         return i
 
-    def vector(r, emit, out, ins, cols=(), two=False):
-        n = width(out)
-        if ins and ins[0][0] == "*":
-            return add(r, "V", emit, ins + list(cols), [out], 50 + G * CY * n, LAT)
-        if two:
-            rate = 1 if any(in_psum(a) for a in ins) else 2
-        else:
-            rate = 0.5 if all(esize(a) == 2 for a in ins + [out]) else 1
-        return add(r, "V", emit, ins + list(cols), [out], max(64, n * rate) * CY + COST["VF"], LAT)
-
     def tt(r, out, a, b, op):
-        return vector(r, lambda g, T: g.vector.tensor_tensor(real(T, out), real(T, a), real(T, b), op), out, [a, b], two=True)
+        return add(r, "V", lambda g, T: g.vector.tensor_tensor(real(T, out), real(T, a), real(T, b), op), [a, b], [out])
 
     def ts(r, out, a, s1, s2, *ops):
-        return vector(r, lambda g, T: g.vector.tensor_scalar(real(T, out), real(T, a), real(T, s1), real(T, s2), *ops),
-                      out, [a], [s for s in (s1, s2) if isinstance(s, tuple)])
+        return add(r, "V", lambda g, T: g.vector.tensor_scalar(real(T, out), real(T, a), real(T, s1), real(T, s2), *ops),
+                   [a] + [s for s in (s1, s2) if isinstance(s, tuple)], [out])
 
     def cp(r, out, a):
-        return vector(r, lambda g, T: g.vector.tensor_copy(real(T, out), real(T, a)), out, [a])
+        return add(r, "V", lambda g, T: g.vector.tensor_copy(real(T, out), real(T, a)), [a], [out])
 
     def const(r, out, v):
-        return vector(r, lambda g, T: g.vector.memset(real(T, out), v), out, [])
+        return add(r, "V", lambda g, T: g.vector.memset(real(T, out), v), [], [out])
 
     def act(r, out, a, func=AF.Copy, scale=None, bias=0.0):
         def emit(g, T):
             if scale is None:
                 return g.scalar.activation(real(T, out), real(T, a), func)
             return g.scalar.activation(real(T, out), real(T, a), func, bias=bias, scale=scale)
-        if a[0] == "*":
-            return add(r, "A", emit, [a], [out], 65 + G * CY * width(out), LAT)
-        return add(r, "A", emit, [a], [out], max(64, width(out)) * CY + COST["AF"], LAT)
+        return add(r, "A", emit, [a], [out])
 
     def mm(r, out, pairs, more=False, end=True):
         def emit(g, T):
             for n, (l, x) in enumerate(pairs):
                 last = g.tensor.matmul(real(T, out), real(T, l), real(T, x), n == 0 and not more, end and n == len(pairs) - 1)
             return last
-        busy = sum(max(64, width(x)) * PE * (4 if esize(x) == 4 else 1) + COST["MF"] for l, x in pairs)
-        return add(r, "P", emit, [a for p in pairs for a in p], [out], busy, LAT + 40)
+        return add(r, "P", emit, [a for p in pairs for a in p], [out])
 
     def iota(r, out, pattern, base, mult):
         def emit(g, T):
             if SCRATCH[out[0]][2] == "int32":
                 return g.iota(real(T, out), pattern, base, mult)
             return g.iota(real(T, out), pattern, base, mult, allow_small_or_imprecise_dtypes=True)
-        return add(r, "G", emit, [], [out], 130 + 2 * CY * width(out), LAT)
+        return add(r, "G", emit, [], [out])
 
     def dma(r, out, a, q="S", after=()):
         sem = (new_sem(r), 16)
-        i = add(r, q, lambda g, T: (g.sync if q == "S" else g.scalar).dma_start(real(T, out), real(T, a)), [a], [out],
-                COST["SI"], 0, after=after, sem=("", 0))
+        i = add(r, q, lambda g, T: (g.sync if q == "S" else g.scalar).dma_start(real(T, out), real(T, a)), [a], [out], after=after, sem=("", 0))
         nodes[i]["inc"] = sem
-        took = (a[3] - a[2]) * width(a) * esize(a) / COST["RATE"] * (1 if in_sbuf(a) or in_sbuf(out) else COST["DD"])
-        took += max(16, a[3] - a[2] if a[1] is None else out[3] - out[2]) * COST["ROW"] / 16
-        return add(r, "D", None, [a], [out], took, COST["DMA"], after=[i], sem=sem)
+        return add(r, "D", None, [a], [out], after=[i], sem=sem)
 
-    def send(r, moves, after=()):
+    def send(r, moves):
         have = len(topo.engines(cores[r], cores[moves[0][0]]))
         shares = [1] * len(moves)
         while 2 * sum(shares) <= have:
@@ -222,40 +176,27 @@ def build(cores, topo):
             g.remote_dma_fused(trs, local_sem=T.sem[ls])
             return None
         srcs = [a for d, out, a in moves]
-        took = [(128 * width(a) * esize(a) * 16 / COST["RR"] + (128 if in_sbuf(a) or in_sbuf(out) else c) * COST["ROW"]) / c
-                for (d, out, a), c in zip(moves, shares)]
-        i = add(r, "G", emit, srcs, [], COST["CALL"], 0.0 if r in sent else COST["FIRST"], after=after, sem=("", 0))
-        sent.add(r)
-        j = add(r, "D", None, [], [], max(took), 0, after=[i], sem=("", 0))
+        i = add(r, "G", emit, srcs, [], sem=("", 0))
+        j = add(r, "D", None, [], [], after=[i], sem=("", 0))
         for (d, out, a, m, s), c in zip(plan, shares):
-            add(d, None, None, [], [out], 0, COST["FAR"] + 200, after=[j], sem=(s, c))
-        add(r, None, None, srcs, [], 0, COST["FAR"], after=[j], sem=(ls, sum(shares)))
+            add(d, None, None, [], [out], after=[j], sem=(s, c))
+        add(r, None, None, srcs, [], after=[j], sem=(ls, sum(shares)))
         return i
 
     def gone(r):
-        return [i for i, v in enumerate(nodes) if v["r"] == r and v["eng"] is None and v["name"] == "send"][-1:]
+        return [i for i, v in enumerate(nodes) if v["r"] == r and v["left"]][-1:]
 
-    def behind(i):
-        nodes[i]["soft"] += [j for j, v in enumerate(nodes[:i]) if (v["r"], v["eng"]) == (nodes[i]["r"], nodes[i]["eng"])]
-
-    def turn(v):
-        lead[0] = -1e5 * v
-
-    def follow(made, lists):
-        for lst in lists:
-            for j in range(2, len(lst), 2):
-                nodes[made[lst[j:j + 2]]]["soft"].append(made[lst[j - 2:j]])
-
-    col = lambda name, j: ap(name, j, j + 1)
+    one = lambda name, j: ap(name, j, j + 1)
     mat = lambda name: ap(name, 0, 128)
     gates = {}
+    cuts = [0]
+    for v in PAR["fin"]:
+        cuts.append(cuts[-1] + sum(n for p, n in pieces(v)))
 
     for r in range(N):
-        ld, made = [], [len(nodes)]
-        turn(-2)
+        ld = []
         dma(r, mat("C0"), mat("c0"), q="A")
         for what in PAR["load"][r].split():
-            made.append(len(nodes))
             if what == "th":
                 dma(r, ap("TH", 0, 640), ap("th", 0, 640))
             elif what == "xb":
@@ -265,54 +206,49 @@ def build(cores, topo):
                 ld.append(dma(r, ap("X", a, b), ap("x", a, b)))
                 if r + 1 < N:
                     send(r, [(r + 1, ap("TAB", a, b), ap("X", a, b))])
-        for a, b in zip(made, made[1:]):
-            nodes[b]["soft"] += [a] if a != made[0] else []
-            nodes[b + 1]["soft"].append(a + 1)
         gates[r] = ld + gone(r)
-    turn(0)
     for r in range(N):
-        for a in (W, 2 * W) if r == 0 else ():
-            gates[r].append(dma(r, ap("TAB", a, min(a + W, WIN)), ap("xb", 0, min(W, WIN - a))))
-        for a in (W, 2 * W) if r + 1 < N else ():
-            behind(send(r, [(r + 1, ap("TAB", a, min(a + W, WIN)), ap("X", 0, min(W, WIN - a)))]))
+        for what in PAR["repeats"][r].split():
+            a = W * int(what[1])
+            n = min(W, WIN - a)
+            if what[0] == "h":
+                gates[r].append(dma(r, ap("TAB", a, a + n), ap("xb", 0, n)))
+            elif what[0] == "v":
+                cp(r, ap("TAB", a, a + n), ap("TAB", 0, n))
+            else:
+                send(r, [(r + 1, ap("TAB", a, a + n), ap("X", 0, n))])
         gates[r] += gone(r)
     for r in range(N):
-        iota(r, col("PI", 0), [[0, 1]], 0, 1)
+        iota(r, one("PI", 0), [[0, 1]], 0, 1)
         iota(r, ap("JR", 0, 144), [[1, 144]], 0, 0)
-        cp(r, col("PF", 0), col("PI", 0))
+        cp(r, one("PF", 0), one("PI", 0))
         for j, m in ((1, 31), (2, 112), (4, 32)):
-            ts(r, col("PI", j), col("PI", 0), m, None, OP.bitwise_and)
-        ts(r, col("PF", 2), col("PI", 2), 15.0, None, OP.add)
-        ts(r, ap("BB", 0, 144), ap("JR", 0, 144), col("PF", 2), UP, OP.is_equal, OP.mult)
-        ts(r, mat("ID"), mat("JR"), col("PF", 0), None, OP.is_equal)
+            ts(r, one("PI", j), one("PI", 0), m, None, OP.bitwise_and)
+        ts(r, one("PF", 2), one("PI", 2), 15.0, None, OP.add)
+        ts(r, ap("BB", 0, 144), ap("JR", 0, 144), one("PF", 2), UP, OP.is_equal, OP.mult)
+        ts(r, mat("ID"), mat("JR"), one("PF", 0), None, OP.is_equal)
         for name, v in (("U16", UP), ("D16", DOWN)):
             ts(r, mat(name), mat("ID"), v, None, OP.mult)
-        for name, v in (("N2", -2.0), ("P5", 5 * DOWN * UP), ("NU", -UP), ("N5", -5 * DOWN * UP), ("PU", UP), ("UD", UP * DOWN)):
+        for name, v in (("N2", -2.0), ("P5", 5 * DOWN * UP), ("NU", -UP), ("N5", -5 * DOWN * UP), ("PU", UP), ("UD", UP * DOWN), ("I32", 1.0)):
             act(r, mat(name), mat("ID"), AF.Identity, v)
-        for j in range(5):
-            ts(r, ap("WW", 128 * j, 128 * j + 96), ap("ID", 0, 96), 0.0, None, OP.mult)
-        for j in range(4):
-            ts(r, ap("WW", 128 * j + 96, 128 * j + 128), ap("ID", 32 * j, 32 * j + 32), DOWN, None, OP.mult)
         if r in WORKERS:
-            behind(iota(r, mat("JM"), [[0, 4], [1, 32]], 0, 0))
-            cp(r, col("PF", 1), col("PI", 1))
-            ts(r, mat("LB"), mat("JM"), col("PF", 1), 0.25, OP.is_equal, OP.mult)
+            iota(r, mat("JM"), [[0, 4], [1, 32]], 0, 0)
+            cp(r, one("PF", 1), one("PI", 1))
+            ts(r, mat("LB"), mat("JM"), one("PF", 1), 0.25, OP.is_equal, OP.mult)
             cp(r, mat("L16"), mat("LB"))
             act(r, mat("L32"), mat("LB"))
-            ts(r, col("PF", 4), col("PI", 1), 4.0, 1.0, OP.mult, OP.add)
-            ts(r, col("PF", 5), col("PI", 4), 0.0625, col("PF", 4), OP.mult, OP.add)
-            ts(r, ap("FF", 0, 136), ap("JR", 0, 136), col("PF", 5), 0.25, OP.is_equal, OP.mult)
+            ts(r, one("PF", 4), one("PI", 1), 4.0, 1.0, OP.mult, OP.add)
+            ts(r, one("PF", 5), one("PI", 4), 0.0625, one("PF", 4), OP.mult, OP.add)
+            ts(r, ap("FF", 0, 136), ap("JR", 0, 136), one("PF", 5), 0.25, OP.is_equal, OP.mult)
 
-    tag[0] = "xr"
     for r in range(N):
         for src, stage, slot in ([("tb", "TD", 4)] if r == 0 else []) + [("x", "XD", r)]:
             moves = []
             for k, d in enumerate(WORKERS):
                 rows = lambda a, b: ap(src, a, b, p0=32 * k, p1=32 * k + 32)
                 if r == N - 1:
-                    for b in range(2):
-                        dst = ap("XC", 256 * b, 256 * b + 256) if d == r else ap(stage, 256 * b, 256 * b + 256, lead=k)
-                        dma(r, dst, rows(1024 * b, 1024 * b + 1024), after=gates[r])
+                    for a, b in zip(cuts, cuts[1:]):
+                        dma(r, ap("XC", a, b) if d == r else ap(stage, a, b, lead=k), rows(4 * a, 4 * b), after=gates[r])
                     if d != r:
                         moves.append((d, ap("XC", 0, 512), ap(stage, 0, 512, lead=k)))
                 elif d != r:
@@ -320,23 +256,33 @@ def build(cores, topo):
                     moves.append((d, ap("XL", 0, 512, lead=slot), ap(stage, 0, 512, lead=k)))
             send(r, moves)
     for k, r in enumerate(WORKERS):
-        first, last = gone(r), []
+        first = gone(r)
         for slot, name, src, owner in [(4, "TB", "tb", 0)] + [(t, "XR%d" % t, "x", t) for t in range(4)]:
             for q in range(4):
                 frm = ap(src, 0, W, p0=32 * k, p1=32 * k + 32) if owner == r else ap("XL", 0, 512, lead=slot)
-                i = dma(r, ap(name, 0, W, p0=32 * q, p1=32 * q + 32), frm, after=first)
-                nodes[i - 1]["soft"] += [j - 1 for j in last]
-                last = [i] if q == 0 else last
+                dma(r, ap(name, 0, W, p0=32 * q, p1=32 * q + 32), frm, after=first)
 
-    def blk(name, m, s):
-        return ap(name, 128 * m + 64 * s, 128 * m + 64 * s + 64)
+    loose, chooser = PAR["loose"], PAR["chooser"]
+    blk = lambda name, m, s: ap(name, 128 * m + 64 * s, 128 * m + 64 * s + 64)
+    col = lambda name, j, n=1: ap(name, 128 * j, 128 * (j + n))
+    bit = lambda name, j, n=1: ap(name, 64 * j, 64 * (j + n))
 
-    defer, mix = PAR["defer"], pieces(PAR["mix"])
-    nm = sum(v for p, v in mix if p == "M")
+    def four(r, kk, ps, sb, apart=False):
+        for to, j, c, op in (("AA", 0, 0, OP.min), ("AA", 1, 0, OP.max), (ps, 2, 1, OP.min), (ps, 3, 1, OP.max)):
+            for s in range(2 * apart):
+                tt(r, blk(to, j, s), blk(ps, c, s), bit(kk, 4 * s + 2 * c), op)
+            if not apart:
+                tt(r, col(to, j), col(ps, c), col(kk, 2 * c), op)
+        tt(r, col(sb, 0), col(ps, 2), col("AA", 0), OP.min)
+        tt(r, col(ps, 0), col(ps, 3), col("AA", 1), OP.min)
+        tt(r, col("AA", 2), col(ps, 2), col("AA", 0), OP.max)
+        tt(r, col(sb, 3), col(ps, 3), col("AA", 1), OP.max)
+        tt(r, col(sb, 2), col(ps, 0), col("AA", 2), OP.max)
+        tt(r, col(sb, 1), col(ps, 0), col("AA", 2), OP.min)
+
     for r in range(N):
-        tag[0] = "pre"
-        turn(0)
-        once = PAR["once"][r]
+        kk, own, mix = "KK%d" % r, chooser[r] == r, pieces(PAR["mix"][r])
+        nm = sum(v for p, v in mix if p == "M")
         for s in range(2):
             cp(r, blk("OFF", 0, s), blk("C0", 0, s))
         ts(r, mat("CK"), mat("C0"), float(BASE), 1 / DOWN, OP.add, OP.mult)
@@ -347,156 +293,168 @@ def build(cores, topo):
             mm(r, ap("PS%d" % s, 0, nm), [(ap("BB", 15 - p, 143 - p), ap("SQ", a + p, b, 16)) for p in range(16)])
             ts(r, ap("NB", 64 * s + 64 - nm, 64 * s + 64), ap("PS%d" % s, 0, nm), 1 / UP, -2047.0, OP.mult, OP.add)
         for m in range(5):
-            turn(2 * m + 0.5)
-            ts(r, ap("TF", 128 * m, 128 * m + 128), ap("TH", 128 * m, 128 * m + 128), -1.0, 2048.0, OP.mult, OP.add)
-            const(r, ap("KC", 64 * m, 64 * m + 64), 3.0 * BASE + KEY * (4 * m - 1) - 2048)
-        made = {}
+            ts(r, col("TF", m), col("TH", m), -1.0, 2048.0, OP.mult, OP.add)
+            const(r, bit("KC", m), 3.0 * BASE + KEY * (4 * m - 1) - 2048)
         for m in range(5):
             for s in range(2):
-                tag[0], w = "m%d%d" % (m, s), 2 * m + s
-                o, x0 = 128 * m + 64 * s, 1024 * s
-                pd, p2, pw, py = "PS%d" % s, "PS%d" % (2 + s), "PS%d" % (4 + s), "PS%d" % (6 + s)
-                cut = -4.0 * BASE - 5.0 * KEY * m
-                turn(w - 1)
-                made["h", w] = act(r, blk("HI", m, s), blk("CK", m, s), AF.Identity, 5 * DOWN, cut - 1022.5)
-                turn(w)
-                u = 0
+                o, x0, u = 128 * m + 64 * s, 1024 * s, 0
+                act(r, blk("HI", m, s), blk("CK", m, s), AF.Identity, 5 * DOWN, -4.0 * BASE - 5.0 * KEY * m - 1022.5)
                 for p, n in mix:
                     a, b = x0 + 16 * u, x0 + 16 * (u + n)
                     src = ind(ap("TAB", 0, WIN if m else W), ap("OFF", o + u, o + u + n))
                     if p == "V":
-                        made["vw"[u > 0], w] = tt(r, ap("DIFF", a, b), src, ap("X", a, b), OP.subtract)
-                        made["qr"[u > 0], w] = act(r, ap("SQ", a, b), ap("DIFF", a, b), AF.Square)
+                        tt(r, ap("DIFF", a, b), src, ap("X", a, b), OP.subtract)
+                        act(r, ap("SQ", a, b), ap("DIFF", a, b), AF.Square)
                     else:
-                        ps = ap(p2, 0, 16 * n)
+                        ps = ap("PS%d" % (2 + s), 0, 16 * n)
                         mm(r, ps, [(mat("N2"), ap("X", a, b))], end=False)
-                        made["g", w] = act(r, ap("GA", a, b), src)
-                        made["a", w] = mm(r, ps, [(mat("ID"), ap("GA", a, b))], more=True)
-                        made["m", w] = tt(r, ap("SQ", a, b), ps, ap("GA", a, b), OP.mult)
+                        act(r, ap("GA", a, b), src)
+                        mm(r, ps, [(mat("ID"), ap("GA", a, b))], more=True)
+                        tt(r, ap("SQ", a, b), ps, ap("GA", a, b), OP.mult)
                     u += n
-                jb = lambda name, a=0, b=256: ap(name, 256 * s + a, 256 * s + b)
-                d, z, ck = ap(pd, 0, 64), ap(py, 0, 64), blk("CK", m + 1, s) if m < 4 else jb("C4", 0, 64)
-                made["p", w] = mm(r, d, [(mat("U16"), blk("NB", 0, s)), (mat("P5"), blk("CK", m, s)), (mat("NU"), blk("HI", m, s))], end=False)
-                made["s", w] = mm(r, d, [(ap("BB", 15 - p, 143 - p), ap("SQ", x0 + p, x0 + 1024, 16)) for p in range(16)], more=True)
-                zero = cut + 2048.0
+                d, ck = ap("PS%d" % s, 0, 64), blk("CK", m + 1, s) if m < 4 else blk(kk, 4, s)
+                z, sb = ap("PS%d" % ((4, 7)[s] if r in loose else 4 + s), 0, 64), "PS%d" % (5 + s)
+                mm(r, d, [(mat("U16"), blk("NB", 0, s)), (mat("P5"), blk("CK", m, s)), (mat("NU"), blk("HI", m, s))], end=False)
+                mm(r, d, [(ap("BB", 15 - p, 143 - p), ap("SQ", x0 + p, x0 + 1024, 16)) for p in range(16)], more=True)
+                zero = 2048.0 - 4.0 * BASE - 5.0 * KEY * m
                 if m < 4:
-                    made["o", w + 2] = ts(r, blk("OFF", m + 1, s), d, 1 / UP, zero, OP.mult, OP.add)
-                turn(w + defer[0])
-                made["c", w + 2] = act(r, ck, d, AF.Identity, 1 / (UP * DOWN), (zero + BASE + KEY * (m + 1)) / DOWN)
-                for j in range(1, 4 * (m == 4)):
-                    act(r, jb("C4", 64 * j, 64 * j + 64), d, AF.Identity, 1 / (UP * DOWN), (zero + BASE + KEY * (m + 1)) / DOWN)
-                made["z", w + 2] = mm(r, z, [(mat("N5"), blk("CK", m, s)), (mat("PU"), blk("HI", m, s)), (mat("PU"), ap("KC", 64 * m, 64 * m + 64)),
-                                             (mat("U16"), blk("TF", m, s)), (mat("UD"), ck)])
-                turn(w + (defer[1] if m < 4 else defer[2]))
-                ws, wp = blk("WS", m // 2, s), ap(pw, 64, 128)
+                    ts(r, blk("OFF", m + 1, s), d, 1 / UP, zero, OP.mult, OP.add)
+                act(r, ck, d, AF.Identity, 1 / (UP * DOWN), (zero + BASE + KEY * (m + 1)) / DOWN)
+                pairs = [(mat("N5"), blk("CK", m, s)), (mat("PU"), blk("HI", m, s)), (mat("PU"), bit("KC", m)),
+                         (mat("U16"), blk("TF", m, s)), (mat("UD"), ck)]
                 if m == 4:
-                    tag[0] = "sel%d" % s
-                lt = lambda j, n=1: jb("LT", 64 * j, 64 * (j + n))
-                cuts = [(0, 256, ap(p2, 256, 512))] if once else [(0, 128, ap(p2, 256, 384)), (128, 256, ap(pw, 0, 128))]
-                if m == 4:
-                    for a, b, keyed in cuts:
-                        tt(r, keyed, ap(pw, 192 + a, 192 + b), jb("C4", a, b), OP.min)
-                tt(r, ws if m in (0, 2) else lt(0) if m == 4 else wp, z, blk("CK", m, s), OP.max)
-                aa = lambda a, b: ap("AA", 128 * s + a, 128 * s + b)
-                if m == 1:
-                    tt(r, aa(0, 64), wp, ws, OP.min)
-                    tt(r, aa(64, 128), wp, ws, OP.max)
-                if m == 3:
-                    tt(r, ap(pw, 384, 448), wp, ws, OP.min)
-                    tt(r, ap(pw, 448, 512), wp, ws, OP.max)
-                    tt(r, ap(pw, 192, 320), ap(pw, 384, 512), aa(0, 128), OP.min)
-                    tt(r, ws, ap(pw, 384, 448), aa(0, 64), OP.max)
-                    tt(r, ap(pw, 384, 448), ap(pw, 448, 512), aa(64, 128), OP.max)
-                    tt(r, ap(pw, 320, 384), ap(pw, 256, 320), ws, OP.max)
-                    tt(r, ap(pw, 256, 320), ap(pw, 256, 320), ws, OP.min)
-                if m == 4:
-                    for j in range(3):
-                        tt(r, lt(j + 1), ap(pw, 192 + 64 * j, 256 + 64 * j), lt(0), OP.max)
-                    for a, b, keyed in cuts:
-                        tt(r, keyed, keyed, lt(a // 64, (b - a) // 64), OP.min)
-                    for a, b, keyed in cuts:
-                        act(r, jb("JK", a, b), keyed, AF.Identity, 1.0, -1023.5 / DOWN)
-                        tt(r, jb("JH", a, b), keyed, jb("JK", a, b), OP.subtract)
-                    perm = lambda k, q: ap("WW", 128 * k + 96 - 32 * q, 128 * k + 224 - 32 * q)
-                    for part in ([range(4)] if once else PAR["parts"][s]):
-                        moves = []
-                        for k in part:
-                            bank, c = ("PS6", 128 * k + 64 * s) if once else (py if 3 in part else pd, 64 * k)
-                            if r < N - 1:
-                                mm(r, ap(bank, c, c + 64), [(perm(k, q), jb("JH", 64 * q, 64 * q + 64)) for q in range(4)])
-                            else:
-                                for u in range(2):
-                                    at = lambda q: 64 * (2 * (q // 2) + u) + 32 * (q % 2)
-                                    mm(r, ap(bank, c + 32 * u, c + 32 * u + 32), [(perm(k, q), jb("JH", at(q), at(q) + 32)) for q in range(4)])
-                            moves += [(WORKERS[k], blk("OFT", r, s), jb("JS", 64 * k, 64 * k + 64))] if WORKERS[k] != r else []
-                        if not once:
-                            far = [k for k in part if WORKERS[k] != r]
-                            cp(r, jb("JS", 64 * far[0], 64 * far[-1] + 64), ap(bank, 64 * far[0], 64 * far[-1] + 64))
-                            send(r, moves)
-                            for k in set(part) - set(far):
-                                cp(r, blk("OFT", r, s), ap(bank, 64 * k, 64 * k + 64))
-                    if once and s == 1:
-                        cp(r, ap("JS", 0, 512), ap("PS6", 0, 512))
-                        send(r, [(d2, ap("OFT", 128 * r, 128 * r + 128), ap("JS", 128 * k, 128 * k + 128)) for k, d2 in enumerate(WORKERS) if d2 != r])
-        mine = [i for i, v in enumerate(nodes) if v["r"] == r and v["eng"] == "V"]
-        for i in mine:
-            if nodes[i]["tag"] == "sel1":
-                nodes[i]["soft"] += [j for j in mine if nodes[j]["tag"] == "sel0"][:PAR["first"][r]]
-        for lst in PAR["beat"]:
-            last = []
-            for w in range(12):
-                for ch, back in pieces(lst):
-                    if (ch, w + 1 - back) in made:
-                        nodes[made[ch, w + 1 - back]]["soft"] += last
-                        last = [made[ch, w + 1 - back]]
+                    mm(r, z, pairs[:4], end=False)
+                mm(r, z, pairs[4 * (m == 4):], more=m == 4)
+                if r in loose:
+                    tt(r, bit(sb, 4) if m % 2 else blk(kk, 5, s) if m == 4 else bit("AA", s), z, blk("CK", m, s), OP.max)
+                    if m % 2:
+                        tt(r, bit(sb, m // 2), bit(sb, 4), bit("AA", s), OP.min)
+                        tt(r, bit("AA", 2 + s) if m == 1 else bit(sb, 5), bit(sb, 4), bit("AA", s), OP.max)
+                    if m == 3:
+                        tt(r, bit(sb, 2), bit(sb, 5), bit("AA", 2 + s), OP.min)
+                        tt(r, bit(sb, 3), bit(sb, 5), bit("AA", 2 + s), OP.max)
+                else:
+                    tt(r, blk("PS7", m // 2, s) if m % 2 else blk(kk, m + (m == 4), s), z, blk("CK", m, s), OP.max)
+                    if (m, s) == (3, 1):
+                        four(r, kk, "PS7", "PS6" if own else kk)
+                        if not own:
+                            send(r, [(chooser[r], col(kk, 0, 4), col(kk, 0, 4))])
+                    if (m, s) == (4, 1) and not own:
+                        send(r, [(chooser[r], col(kk, 4, 2), col(kk, 4, 2))])
 
-    def parents_out(r):
-        tag[0] = "yj"
-        for s in range(2):
-            for q in range(4):
-                mm(r, blk("PS7", q, s), [(mat("D16"), ap("JH", 256 * s + 64 * q, 256 * s + 64 * q + 64))])
-        act(r, ap("YJ", 0, 512), ap("PS7", 0, 512))
-        dma(r, ap("yj", 0, 512), ap("YJ", 0, 512), after=gone(r))
+    def move(r, items):
+        trip = [(ap(pb, c, c + n, p0=32 * q, p1=32 * q + 32), ap("D16", 32 * k, 32 * k + 32), ap(jh, a, a + n)) for pb, c, n, k, q, jh, a in items]
 
-    def lists(r, t, a, b):
-        if t == r and PAR["once"][r]:
-            base = 128 * WORKERS.index(r) + a
-            return ap("JS", base, base + b - a)
+        def emit(g, T):
+            for out, l, x in trip:
+                last = g.tensor.matmul(real(T, out), real(T, l), real(T, x), True, True)
+            return last
+        return add(r, "P", emit, [a for v in trip for a in v[1:]], [v[0] for v in trip])
+
+    def plain(r, jh, sb, a, b, c):
+        act(r, ap("JK", c, c + b - a), ap(sb, a, b), AF.Identity, 1.0, -1023.5 / DOWN)
+        tt(r, ap(jh, c, c + b - a), ap(sb, a, b), ap("JK", c, c + b - a), OP.subtract)
+
+    def deal(t, pb, a, n, base):
+        r = chooser[t]
+        far = [k for k in range(4) if WORKERS[k] != r]
+        js = lambda u, v: ap("JS", 512 * t + base + u, 512 * t + base + v)
+        if far == list(range(far[0], far[-1] + 1)):
+            cp(r, js(n * far[0], n * far[-1] + n), ap(pb, n * far[0], n * far[-1] + n))
+        else:
+            cp(r, js(0, 4 * n), ap(pb, 0, 4 * n))
+        send(r, [(WORKERS[k], ap("OFT", 128 * t + a, 128 * t + a + n), js(n * k, n * k + n)) for k in far])
+        for k in set(range(4)) - set(far):
+            cp(r, ap("OFT", 128 * t + a, 128 * t + a + n), ap(pb, n * k, n * k + n))
+
+    def quick(t, s, sb, pb):
+        kk, jh = "KK%d" % t, "JH%d" % t
+        n = PAR["ahead"][t][s]
+        for j in range(4):
+            tt(t, bit(sb, j), bit(sb, j), blk(kk, 4, s), OP.min)
+        if n:
+            act(t, bit("JK", 4 * s, n), bit(sb, 0, n), AF.Identity, 1.0, -1023.5 / DOWN)
+        tt(t, bit(sb, 3), bit(sb, 3), blk(kk, 5, s), OP.min)
+        if n:
+            tt(t, bit(jh, 4 * s, n), bit(sb, 0, n), bit("JK", 4 * s, n), OP.subtract)
+        plain(t, jh, sb, 64 * n, 256, 256 * s + 64 * n)
+        for q in range(4):
+            move(t, [(pb, 64 * k, 64, k, q, jh, 256 * s + 64 * q) for k in range(4)])
+        deal(t, pb, 64 * s, 64, 256 * s)
+        act(t, bit("KL%d" % t, 4 * s, 4), bit(sb, 0, 4))
+        if t and s:
+            send(t, [(0, col("KL%d" % t, 0, 4), col("KL%d" % t, 0, 4))])
+
+    def late(t, sb, pb):
+        r, kk, jh = chooser[t], "KK%d" % t, "JH%d" % t
+        if r != t:
+            mm(r, col(sb, 0, 4), [(mat("I32"), col(kk, 0, 4))])
+        for j in range(4):
+            tt(r, col(sb, j), col(sb, j), col(kk, 4), OP.min)
+        for j in range(3):
+            tt(r, col(kk, 6 + j), col(sb, j), col(kk, 5), OP.max)
+        tt(r, col(sb, 0, 4), col(sb, 0, 4), col(kk, 5, 4), OP.min)
+        plain(r, jh, sb, 0, 512, 0)
+        for q in range(4):
+            if t < N - 1:
+                move(r, [(pb, 128 * k, 128, k, q, jh, 128 * q) for k in range(4)])
+            else:
+                move(r, [(pb, 128 * k + a // 4 + (b - a) // 8 * u, (b - a) // 8, k, q, jh, 128 * (2 * (q // 2) + u) + a // 4 + (b - a) // 8 * (q % 2))
+                         for k in range(4) for a, b in zip(cuts, cuts[1:]) for u in range(2)])
+        deal(t, pb, 0, 128, 0)
+
+    outs = []
+    for what in PAR["choose"].split():
+        t, (sb, pb) = int(what[1]), ["PS" + v for v in what[-2:]]
+        r, yj = chooser[t], ap("YJ%d" % t, 0, 512)
+        if what[0] == "q":
+            quick(t, int(what[2]), sb, pb)
+            continue
+        if what[0] == "l":
+            late(t, sb, pb)
+            mm(r, col(sb, 0, 4), [(mat("D16"), col("JH%d" % t, 0, 4))])
+            act(r, yj, col(sb, 0, 4))
+        else:
+            r, kl = 0, "KL%d" % t
+            for j in range(4):
+                mm(r, bit(pb, j), [(mat("I32"), bit(kl, 4 * (j % 2) + j // 2 * 2 + 1))])
+            four(r, kl, pb, sb, True)
+            plain(r, "JL", sb, 0, 512, 0)
+            act(r, yj, col("JL", 0, 4), AF.Identity, DOWN)
+        if r != t:
+            send(r, [(t, yj, yj)])
+        outs.append((t, yj))
+
+    def lists(t, a, b):
         return ap("OFT", 128 * t + a, 128 * t + b)
 
     def piece(k, b):
         return ap("ytau", 1024 * b, 1024 * b + 1024, p0=32 * k, p1=32 * k + 32)
 
-    staged, ready, stores = {}, {}, []
+    ready = {}
 
     def hand(r, names):
-        i = send(r, [ready[(r, v)] for v in names])
+        send(r, [ready[(r, v)][:3] for v in names])
         for v in names:
-            d, out, a = ready[(r, v)]
-            stores.append((d, len(nodes)))
-            dma(d, piece(out[1] // 2, out[1] % 2), out, q="A" if d == N - 1 and out[1] // 2 % 2 else "S")
-        return i
+            d, out, a, to = ready[(r, v)]
+            dma(d, to, out, q="A" if d == N - 1 and to[2] // 32 % 2 else "S")
 
-    turn(defer[3])
-    for r in range(N):
-        parents_out(r)
+    for t, yj in outs:
+        dma(t, ap("yj", 0, 512), yj)
     for t in range(4):
         for k, r in enumerate(WORKERS):
-            tag[0] = "t%d" % t
             win = ap("TB" if t == 0 else "T%d" % (t - 1), 0, W)
-            b, made = 0, {}
-            plan = PAR["steps"][t].split()
-            for c, (how, n) in enumerate(pieces(plan[0])):
+            b = 0
+            for c, (how, n) in enumerate(pieces(PAR["steps"][t])):
                 a, b = b, b + 64 * n
-                first = len(nodes)
-                src = ind(win, lists(r, t, a // 16, b // 16))
-                ps = ap("PS" + (PAR["banks"][c] if t == 0 else str(c % 8)), 0, b - a)
+                src = ind(win, lists(t, a // 16, b // 16))
+                ps = ap("PS" + (PAR["banks"][r][c] if t == 0 else str(c % 8)), 0, b - a)
                 xr, out = ap("XR%d" % t, a, b), ap("T%d" % t, a, b)
                 if how == "D":
                     gb = ap("G16" if t < 2 else "G32", a, b)
                     tt(r, gb, src, xr, OP.add)
                     pairs = [(mat("L16" if t < 2 else "L32"), gb)]
-                elif how == "A":
+                elif how in "AB":
                     gb = ap("GH" if t == 0 else "G32", a, b)
                     act(r, gb, src)
                     pairs = [(mat("LB" if t == 0 else "L32"), gb)]
@@ -504,180 +462,94 @@ def build(cores, topo):
                     act(r, ap("GH", a, b), src)
                     tt(r, ap("GL", a, b), src, ap("GH", a, b), OP.subtract)
                     pairs = [(mat("LB"), ap("GH", a, b)), (mat("LB"), ap("GL", a, b))]
-                mm(r, ps, pairs)
-                if how == "D":
+                if how in "BT":
+                    mm(r, ps, [(mat("LB"), xr)], end=False)
+                mm(r, ps, pairs, more=how in "BT")
+                if how in "DBT":
                     act(r, out, ps)
                 else:
                     tt(r, out, ps, xr, OP.add)
-                for i, v in zip(range(first, len(nodes)), "hlpe" if how == "S" else "gpe"):
-                    made[v + str(c)] = i
-            follow(made, plan[1:])
-            if t == r == 0:
-                for i in made.values():
-                    nodes[i]["soft"] += [j for j, v in enumerate(nodes) if v["r"] == r and v["tag"][:3] == "sel" and v["eng"] == nodes[i]["eng"]]
-            tag[0] = "o%d" % t
             for b in range(2):
-                staged[(r, t, b)] = len(nodes)
                 dma(r, piece(k, b) if r == t else ap("OD", 0, 256, lead=2 * t + b), ap("T%d" % t, 1024 * b, 1024 * b + 1024, p1=32))
-                ready[(r, "ab"[b])] = (t, ap("LD", 0, 256, lead=2 * k + b), ap("OD", 0, 256, lead=2 * t + b))
+                ready[(r, "ab"[b])] = (t, ap("LD", 0, 256, lead=2 * k + b), ap("OD", 0, 256, lead=2 * t + b), piece(k, b))
             if r != t and t < 3:
                 hand(r, "ab")
-        for (d, i) in stores:
-            if (d, t, 1) in staged and d + 1 == t:
-                nodes[i]["soft"] += [staged[(d, t, 0)], staged[(d, t, 1)]]
-    t, made = N - 1, [{} for r in range(N)]
-    for b in range(2):
+    t, num = N - 1, 0
+    for b, (c0, c1) in enumerate(zip(cuts, cuts[1:])):
         for k, r in enumerate(WORKERS):
-            tag[0] = "t4"
-            win, c = ap("T3", 0, W), 0
+            win, c, wd = ap("T3", 0, W), 0, c1 - c0
             for j, (how, n) in enumerate(pieces(PAR["fin"][b])):
-                xc, ps = ap("XC", 256 * b + c, 256 * b + c + n), ap("PS%d" % (4 * b + j), 0, n)
+                xc, ps = ap("XC", c0 + c, c0 + c + n), ap("PS%d" % (num + j), 0, n)
                 pairs = [(mat("ID"), xc)] if how == "P" else []
-                num = len(pieces(PAR["fin"][0])) * b + j
                 for jj in range(2):
-                    a, lc = 512 * b + 256 * jj + c, 64 * b + 16 * jj + c // 16
-                    ga, gv, at = ap("G32", a, a + n), ap("G32", 1024 + a, 1024 + a + n), str(2 * num + jj)
-                    made[r]["a" + at] = act(r, ga, ind(win, lists(r, t, lc, lc + n // 16)))
-                    made[r]["v" + at] = tt(r, gv, ind(win, lists(r, t, lc + 32, lc + 32 + n // 16)), ga, OP.add)
-                    made[r]["p" + at] = mm(r, ps, pairs + [(ap("FF", 1 - jj, 129 - jj), gv)], more=jj == 1, end=jj == 1)
+                    a, lc = 2 * c0 + wd * jj + c, c0 // 4 + (wd * jj + c) // 16
+                    ga, gv = ap("G32", a, a + n), ap("G32", 1024 + a, 1024 + a + n)
+                    (cp if 2 * (num + j) + jj in PAR["solo"] else act)(r, ga, ind(win, lists(t, lc, lc + n // 16)))
+                    tt(r, gv, ind(win, lists(t, lc + wd // 8, lc + wd // 8 + n // 16)), ga, OP.add)
+                    mm(r, ps, pairs + [(ap("FF", 1 - jj, 129 - jj), gv)], more=jj == 1, end=jj == 1)
                     pairs = []
-                fin = ap("FIN", 256 * b + c, 256 * b + c + n)
-                made[r]["e" + str(num)] = act(r, fin, ps) if how == "P" else tt(r, fin, ps, xc, OP.add)
+                fin = ap("FIN", c0 + c, c0 + c + n)
+                if how == "P":
+                    act(r, fin, ps)
+                else:
+                    tt(r, fin, ps, xc, OP.add)
                 c += n
-            tag[0] = "o4"
-            ready[(r, "fg"[b])] = (t, ap("LD", 0, 256, lead=2 * k + b), ap("FIN", 256 * b, 256 * b + 256))
+            to = ap("ytau", 4 * c0, 4 * c1, p0=32 * k, p1=32 * k + 32)
+            ready[(r, "fghi"[b])] = (t, ap("L%d" % wd, 0, wd, lead=4 * b + k), ap("FIN", c0, c1), to)
             if r == t:
-                dma(r, piece(k, b), ap("FIN", 256 * b, 256 * b + 256))
+                dma(r, to, ap("FIN", c0, c1))
+        num += len(pieces(PAR["fin"][b]))
     for r in WORKERS:
-        last = []
         for names in PAR["last"][r].split():
-            i = hand(r, names)
-            nodes[i]["soft"], last = last, [i]
-        follow(made[r], PAR["fin"][2:])
+            hand(r, names)
     return nodes
 
 
-def rising(links, back, key):
-    key, left = list(key), [len(b) for b in links[back]]
-    todo = [i for i, c in enumerate(left) if not c]
-    while todo:
-        i = todo.pop()
-        for u, gap in links[1 - back][i]:
-            key[u] = max(key[u], key[i] + 1e-3)
+def line_up(nodes):
+    n = len(nodes)
+    before = [set(v["deps"]) for v in nodes]
+    for name, code in ORDER.items():
+        rest, skip, last = [i for i, v in enumerate(nodes) if (v["r"], v["eng"]) == (int(name[0]), name[1])], 0, []
+        for ch in code + "0" * len(rest):
+            skip += LETTERS.index(ch)
+            if rest and ch != LETTERS[-1]:
+                i, skip = rest.pop(skip), 0
+                before[i].update(last)
+                last = [i]
+    after = [[] for _ in range(n)]
+    for i in range(n):
+        for d in before[i]:
+            after[d].append(i)
+    left = [len(b) for b in before]
+    seq = [i for i in range(n) if not left[i]]
+    for i in seq:
+        for u in after[i]:
             left[u] -= 1
             if not left[u]:
-                todo.append(u)
-    return sorted(range(len(key)), key=lambda i: (key[i], i))
+                seq.append(u)
+    assert len(seq) == n
+    return seq
 
 
-def place(nodes, links, key, back):
-    end, used = [0.0] * len(nodes), {}
-    for i in rising(links, back, key):
+def waits(nodes, seq):
+    mark, count, place = {}, {}, {}
+    for p, i in enumerate(seq):
         v = nodes[i]
-        t = max([v["lat"] if back else 0.0] + [end[d] + gap for d, gap in links[back][i]])
-        if v["eng"]:
-            lst = used.setdefault((v["r"], v["eng"]), [])
-            j = len(lst)
-            while j and lst[j - 1][1] > t:
-                j -= 1
-            while j < len(lst) and lst[j][0] < t + v["busy"]:
-                t = max(t, lst[j][1])
-                j += 1
-            lst.insert(j, (t, t + v["busy"]))
-        end[i] = t + v["busy"]
-    return end
-
-
-def greedy(nodes, links):
-    n = len(nodes)
-    way = [0.0] * n
-    for i in rising(links, 1, [0.0] * n):
-        way[i] = nodes[i]["busy"] + max([nodes[i]["lat"]] + [way[u] + gap for u, gap in links[1][i]])
-    left, at, end = [len(b) for b in links[0]], [0.0] * n, [0.0] * n
-    free, ready = {}, {}
-
-    def finish(i, t0):
-        end[i] = t0 + nodes[i]["busy"]
-        for u, gap in links[1][i]:
-            at[u] = max(at[u], end[i] + gap)
-            left[u] -= 1
-            if left[u] == 0:
-                release(u)
-
-    def release(i):
-        if nodes[i]["eng"] is None:
-            finish(i, at[i])
+        place[i] = p
+        if v["sem"] is None:
+            count[(v["r"], v["eng"])] = count.get((v["r"], v["eng"]), 0) + 1
+            mark[i] = ("c" + v["eng"], count[(v["r"], v["eng"])])
         else:
-            ready.setdefault((nodes[i]["r"], nodes[i]["eng"]), []).append(i)
-
-    for i in [i for i in range(n) if not left[i]]:
-        release(i)
-    while True:
-        soon = [(max(free.get(q, 0.0), min(at[i] for i in lst)), q) for q, lst in ready.items() if lst]
-        if not soon:
-            return end
-        t0, q = min(soon)
-        i = max((i for i in ready[q] if at[i] <= t0), key=lambda i: (way[i] + nodes[i]["lead"], -i))
-        ready[q].remove(i)
-        free[q] = t0 + nodes[i]["busy"]
-        finish(i, t0)
-
-
-def hop(a, b):
-    if a["eng"] == b["eng"] == "P":
-        return 0.0
-    return a["lat"] + ((COST["HS"] if a["eng"] == b["eng"] else COST["HOP"]) if b["emit"] else 0.0)
-
-
-def schedule(nodes):
-    n = len(nodes)
-    soft = [list(v["soft"]) for v in nodes]
-    for q, code in ORDER.items():
-        rest, skip, last = [i for i, v in enumerate(nodes) if (v["r"], v["eng"]) == q], 0, []
-        for ch in code:
-            skip += LETTERS.index(ch)
-            if ch != LETTERS[-1]:
-                i, skip = rest.pop(skip), 0
-                soft[i], last = last, [i]
-    links = ([[] for _ in range(n)], [[] for _ in range(n)])
-    for i, v in enumerate(nodes):
-        for d, gap in [(d, hop(nodes[d], v)) for d in sorted(v["deps"])] + [(d, 0.0) for d in soft[i]]:
-            links[0][i].append((d, gap))
-            links[1][d].append((i, gap))
-    end, best = greedy(nodes, links), None
-    for _ in range(5):
-        span = max(e + v["lat"] for e, v in zip(end, nodes)) + 0.2 * sum(end) / n
-        if best is None or span < best[0]:
-            best = (span, end)
-        end = place(nodes, links, [-e for e in place(nodes, links, [-e for e in end], 1)], 0)
-    start = [e - v["busy"] for e, v in zip(best[1], nodes)]
-    order = {}
-    for i in sorted(range(n), key=lambda i: (start[i], i)):
-        if nodes[i]["eng"]:
-            order.setdefault((nodes[i]["r"], nodes[i]["eng"]), []).append(i)
-    return order, start, [e + v["lat"] for e, v in zip(best[1], nodes)]
-
-
-def waits(nodes, order, start):
-    mark = {}
-    for (r, eng), lst in order.items():
-        c = 0
-        for i in lst:
-            if nodes[i]["sem"] is None:
-                c += 1
-                mark[i] = ("c" + eng, c)
-    for i, v in enumerate(nodes):
-        if v["sem"] is not None:
             mark[i] = v["sem"]
     known, clock, need = {}, {}, {}
-    for i in sorted(range(len(nodes)), key=lambda i: (start[i], i)):
+    for i in seq:
         v = nodes[i]
         if v["emit"] is None:
             clock[i] = {}
             continue
         k = known.setdefault((v["r"], v["eng"]), {})
         need[i] = {}
-        for d in sorted(v["deps"], key=lambda d: -start[d]):
+        for d in sorted(v["deps"], key=lambda d: -place[d]):
             name, c = mark[d]
             if name and k.get(name, 0) < c and not (v["eng"] == "P" and name == "cP"):
                 need[i][name] = c
@@ -697,17 +569,18 @@ def rank_program(g, core, T, topo):
         return
     if not PLAN:
         nodes = build(list(T.cores), topo)
-        order, start, done = schedule(nodes)
-        PLAN["all"] = (nodes, order, start, done) + waits(nodes, order, start)
-    nodes, order, start, done, mark, need = PLAN["all"]
+        seq = line_up(nodes)
+        PLAN["all"] = (nodes, seq) + waits(nodes, seq)
+    nodes, seq, mark, need = PLAN["all"]
     queue = {"V": g.vector, "A": g.scalar, "P": g.tensor, "G": g, "S": g.sync}
     top, got = {}, {}
     for i, v in enumerate(nodes):
         if v["r"] == r and mark[i][0]:
             top[mark[i][0]] = max(top.get(mark[i][0], 0), mark[i][1])
-    mine = [i for (r2, eng), lst in order.items() if r2 == r for i in lst if nodes[i]["emit"]]
-    for i in sorted(mine, key=lambda i: (start[i], i)):
+    for i in seq:
         v = nodes[i]
+        if v["r"] != r or not v["emit"]:
+            continue
         for name, c in need[i].items():
             queue[v["eng"]].wait_ge(T.sem[name], c)
             got[name] = max(got.get(name, 0), c)

from concourse.bass import DstId, RemoteDMATransfer
from concourse.mybir import AluOpType as OP
from concourse.mybir import ActivationFunctionType as AF

N = 5
W = 2048
WORKERS = [1, 2, 3, 4]
WIN = 5648
KEY = 8192
BASE = 129 * W
DOWN = 128.0
UP = 4096.0

PAR = {
    "load": ["02 xb 28 th"] + ["02 28 th"] * 3 + ["08 th"],
    "repeats": ["v1 h2 s1 s2", "s1 s2", "s2", "v1 s1 s2", ""],
    "mix": ["V20V20M24"] * 3 + ["V22V20M22"] * 2,
    "loose": [0, 1],
    "ahead": [[0, 3], [0, 0]],
    "chooser": [0, 1, 2, 0, 0],
    "choose": "q0052 q0163 q1052 q1163 l267 l304 l417 s052 s163",
    "steps": ["D8A8D4D5A7", "A3D6A4D3D7A2D4A3", "A1S5S8T3D6D6B2A1", "A1S5S8T3D6D6B2A1"],
    "banks": ["", "014701", "012345", "012345", "012345"],
    "fin": ["p128P128", "p128", "p128"], "solo": [0],
    "last": ["", "f a b g h", "f a b g h", "f g h", "a b"],
}
LETTERS = "0123456789abcdefghijklmnopqrstuvwxyzABCDEFGHIJKLMNOPQRSTUVWXYZ+"
ORDER = {"0A":"0112300b6112112201502115031150211502161031104316101215010101010000101111","0S":"100104434110043433211","0G":"440010000001","1A":"003001511010425102150211501115021150211502115021104110520210001001301006122000721123021072114201101001111","1S":"0002008888cccc88884444000011215443312121","1G":"544001002000021","2A":"0000000000002004111501115021150211503115021104211041105201100024121310341100726112301072150031101001111","2S":"000000cccc888888884444000011000327623311","2G":"43300000002","3A":"01010000121502500210411150311502115031150111043110411600121001300001532000726100121072112430101101111","3S":"000000gggg88888888444400001111110105412","3G":"544001","4A":"00003201110042003110411104111501115021150211501210411052011001301001522000721514201072214201104113011","4S":"00622501230110gggg888888884444000011112121000033001","0V":"32211112abcfd733211077a068075177505a958cc80acca2eacc1181fe271j1a20e1d70d1b0101a7a608760100013332021000020110002422aab081761141304402121655252224313321","3V":"1255331hijkl155111111113541331211141300133125420244236042355023604202ee2g1c0c2b00103211100001100412310106631321006631321000022011201","1V":"05514k0k12j92220f0030355461220101040220331266204884791805688626cc304107dd700dab0491202010602220164503302401432010412300106631321006631321000020111011","2V":"01423202fghij03300000004544400011002201331244202442025420244012440612dd20db0b0a100213110322100200002432204420310006631321006631321100020111011","4G":"0100000001","4V":"0123013ghijk34300410000445540101113300133124401244012442024401254202ee01ee0b20a200113210000210041231200663132110663132100004224012","0P":"77220000411252236122302233304423a30330203120133111000030100100e05abaccb111005011","1P":"2106130203120411220312501125011250112041132500430010002000100000110035000103664421100736442110001","2P":"2001020141120131201312041125011250112013173200330220103303212210201110103664421100736442111001","3P":"260014024012013120131250112520122031204110114420011100000100310021036644211007364421100011","4P":"2600100141120131220312501120131204112501170110331010000011003103010366442111073644211000311"}

SCRATCH = {"XD": ("dram", [4, 128, 512], "bfloat16"), "TD": ("dram", [4, 128, 512], "bfloat16"), "XL": ("dram", [5, 128, 512], "bfloat16"),
           "OD": ("dram", [8, 128, 256], "float32"), "LD": ("dram", [8, 128, 256], "float32"),
           "L128": ("dram", [16, 128, 128], "float32"), "L256": ("dram", [16, 128, 256], "float32")}
for _d, _l in (("bfloat16", "X:2048 TAB:5648 ID:128 N2:128 PU:128 NU:128 BB:144 LB:128 DIFF:2048 SQ:2048 GA:2048 HI:640 KC:320 JK:512 "
                            "TB:2048 XC:512 GH:2048 GL:2048 XR0:2048 XR1:2048 XR2:2048 XR3:2048"),
               ("float32", "JR:144 JM:128 PF:8 L32:128 FF:136 P5:128 N5:128 UD:128 CK:640 I32:128 AA:384 JL:512 KL0:512 KL1:512 "
                           "KK0:1152 KK1:1152 KK2:1152 KK3:1152 KK4:1152 YJ0:512 YJ1:512 YJ2:512 YJ3:512 YJ4:512 FIN:512 "
                           "G32:2048 T0:2048 T1:2048 T2:2048 T3:2048"),
               ("float16", "TF:640 U16:128 D16:128 NB:128 L16:128 JH0:512 JH1:512 JH2:512 JH3:512 JH4:512 G16:2048"),
               ("int32", "C0:128 TH:640 PI:8"), ("uint16", "OFF:640 JS:2560 OFT:640")):
    for _s in _l.split():
        SCRATCH[_s.split(":")[0]] = ("sbuf", [128, int(_s.split(":")[1])], _d)
for _b in range(8):
    SCRATCH["PS%d" % _b] = ("psum", [128, 512], "float32")
SEMAPHORES = ["cV", "cA", "cP", "cG"] + ["s%d" % _i for _i in range(140)]
IO = ("x", "xb", "tb", "c0", "th", "yj", "ytau")


def ap(name, c0, c1, step=1, p0=0, p1=128, lead=None):
    return (name, lead, p0, p1, c0, c1, step)


def ind(win, off):
    return ("*", win, off)


def real(T, a):
    if not isinstance(a, tuple):
        return a
    if a[0] == "*":
        return real(T, a[1]).indirect(real(T, a[2]))
    name, lead, p0, p1, c0, c1, step = a
    if lead is not None:
        if (p0, p1, c0, c1) == (0, 128, 0, SCRATCH[name][1][2]):
            return T[name][lead]
        return T[name][lead, p0:p1, c0:c1]
    if step != 1:
        return T[name][p0:p1, c0:c1:step]
    return T[name][p0:p1, c0:c1]


def pieces(s):
    out = []
    for ch in s:
        if ch.isdigit():
            out[-1][1] = 10 * out[-1][1] + int(ch)
        else:
            out.append([ch, 0])
    return [(a, b) for a, b in out if b]


def build(cores, topo):
    nodes, seen, banks, pool = [], {}, {}, [0] * N

    def new_sem(r):
        pool[r] += 1
        return "s%d" % (pool[r] - 1)

    def add(r, eng, emit, reads, writes, after=(), sem=None):
        i, deps = len(nodes), set(after)
        flat = []
        for a in reads:
            flat += [(a[1], False), (a[2], False)] if a[0] == "*" else [(a, False)]
        flat += [(a, True) for a in writes]
        for a, wr in flat:
            if a[0] in IO:
                continue
            for (b, bw, j) in seen.setdefault((r, a[0], a[1]), []):
                if (wr or bw) and a[2] < b[3] and b[2] < a[3] and a[4] < b[5] and b[4] < a[5]:
                    deps.add(j)
        for name in set(a[0] for a, wr in flat if a[0].startswith("PS")):
            st = banks.setdefault((r, name), [eng, [], []])
            if st[0] != eng:
                st[0], st[1], st[2] = eng, [], st[1]
            st[1].append(i)
            deps.update(st[2])
        for a, wr in flat:
            if a[0] not in IO:
                seen[(r, a[0], a[1])].append((a, wr, i))
        deps.discard(i)
        nodes.append({"r": r, "eng": eng, "emit": emit, "deps": deps, "sem": sem, "left": eng is None and not writes})
        return i

    def tt(r, out, a, b, op):
        return add(r, "V", lambda g, T: g.vector.tensor_tensor(real(T, out), real(T, a), real(T, b), op), [a, b], [out])

    def ts(r, out, a, s1, s2, *ops):
        return add(r, "V", lambda g, T: g.vector.tensor_scalar(real(T, out), real(T, a), real(T, s1), real(T, s2), *ops),
                   [a] + [s for s in (s1, s2) if isinstance(s, tuple)], [out])

    def cp(r, out, a):
        return add(r, "V", lambda g, T: g.vector.tensor_copy(real(T, out), real(T, a)), [a], [out])

    def const(r, out, v):
        return add(r, "V", lambda g, T: g.vector.memset(real(T, out), v), [], [out])

    def act(r, out, a, func=AF.Copy, scale=None, bias=0.0):
        def emit(g, T):
            if scale is None:
                return g.scalar.activation(real(T, out), real(T, a), func)
            return g.scalar.activation(real(T, out), real(T, a), func, bias=bias, scale=scale)
        return add(r, "A", emit, [a], [out])

    def mm(r, out, pairs, more=False, end=True):
        def emit(g, T):
            for n, (l, x) in enumerate(pairs):
                last = g.tensor.matmul(real(T, out), real(T, l), real(T, x), n == 0 and not more, end and n == len(pairs) - 1)
            return last
        return add(r, "P", emit, [a for p in pairs for a in p], [out])

    def iota(r, out, pattern, base, mult):
        def emit(g, T):
            if SCRATCH[out[0]][2] == "int32":
                return g.iota(real(T, out), pattern, base, mult)
            return g.iota(real(T, out), pattern, base, mult, allow_small_or_imprecise_dtypes=True)
        return add(r, "G", emit, [], [out])

    def dma(r, out, a, q="S", after=()):
        sem = (new_sem(r), 16)
        i = add(r, q, lambda g, T: (g.sync if q == "S" else g.scalar).dma_start(real(T, out), real(T, a)), [a], [out], after=after, sem=("", 0))
        nodes[i]["inc"] = sem
        return add(r, "D", None, [a], [out], after=[i], sem=sem)

    def send(r, moves):
        have = len(topo.engines(cores[r], cores[moves[0][0]]))
        shares = [1] * len(moves)
        while 2 * sum(shares) <= have:
            shares = [2 * v for v in shares]
        if sum(shares) + shares[0] <= have:
            shares[0] *= 2
        plan = []
        for n, (d, out, a) in enumerate(moves):
            e = topo.engines(cores[r], cores[d])
            plan.append((d, out, a, sum(1 << v for v in e[sum(shares[:n]):sum(shares[:n + 1])]), new_sem(d)))
        ls = new_sem(r)

        def emit(g, T):
            if len(plan) == 1:
                d, out, a, m, s = plan[0]
                rid, pid, se = topo.addr(cores[d])
                g.remote_dma(real(T, out), real(T, a), T.sem[s], T.sem[ls], pid, rid, m)
                return None
            trs = []
            for d, out, a, m, s in plan:
                rid, pid, se = topo.addr(cores[d])
                trs.append(RemoteDMATransfer(dst_ids=[DstId(rid=rid, pnc=pid)], dma_engine_mask=m, remote_sem=T.sem[s], src=real(T, a), dst=real(T, out)))
            g.remote_dma_fused(trs, local_sem=T.sem[ls])
            return None
        srcs = [a for d, out, a in moves]
        i = add(r, "G", emit, srcs, [], sem=("", 0))
        j = add(r, "D", None, [], [], after=[i], sem=("", 0))
        for (d, out, a, m, s), c in zip(plan, shares):
            add(d, None, None, [], [out], after=[j], sem=(s, c))
        add(r, None, None, srcs, [], after=[j], sem=(ls, sum(shares)))
        return i

    def gone(r):
        return [i for i, v in enumerate(nodes) if v["r"] == r and v["left"]][-1:]

    one = lambda name, j: ap(name, j, j + 1)
    mat = lambda name: ap(name, 0, 128)
    gates = {}
    cuts = [0]
    for v in PAR["fin"]:
        cuts.append(cuts[-1] + sum(n for p, n in pieces(v)))

    for r in range(N):
        ld = []
        dma(r, mat("C0"), mat("c0"), q="A")
        for what in PAR["load"][r].split():
            if what == "th":
                dma(r, ap("TH", 0, 640), ap("th", 0, 640))
            elif what == "xb":
                ld.append(dma(r, ap("TAB", 0, W), ap("xb", 0, W)))
            else:
                a, b = [256 * int(v) for v in what]
                ld.append(dma(r, ap("X", a, b), ap("x", a, b)))
                if r + 1 < N:
                    send(r, [(r + 1, ap("TAB", a, b), ap("X", a, b))])
        gates[r] = ld + gone(r)
    for r in range(N):
        for what in PAR["repeats"][r].split():
            a = W * int(what[1])
            n = min(W, WIN - a)
            if what[0] == "h":
                gates[r].append(dma(r, ap("TAB", a, a + n), ap("xb", 0, n)))
            elif what[0] == "v":
                cp(r, ap("TAB", a, a + n), ap("TAB", 0, n))
            else:
                send(r, [(r + 1, ap("TAB", a, a + n), ap("X", 0, n))])
        gates[r] += gone(r)
    for r in range(N):
        iota(r, one("PI", 0), [[0, 1]], 0, 1)
        iota(r, ap("JR", 0, 144), [[1, 144]], 0, 0)
        cp(r, one("PF", 0), one("PI", 0))
        for j, m in ((1, 31), (2, 112), (4, 32)):
            ts(r, one("PI", j), one("PI", 0), m, None, OP.bitwise_and)
        ts(r, one("PF", 2), one("PI", 2), 15.0, None, OP.add)
        ts(r, ap("BB", 0, 144), ap("JR", 0, 144), one("PF", 2), UP, OP.is_equal, OP.mult)
        ts(r, mat("ID"), mat("JR"), one("PF", 0), None, OP.is_equal)
        for name, v in (("U16", UP), ("D16", DOWN)):
            ts(r, mat(name), mat("ID"), v, None, OP.mult)
        for name, v in (("N2", -2.0), ("P5", 5 * DOWN * UP), ("NU", -UP), ("N5", -5 * DOWN * UP), ("PU", UP), ("UD", UP * DOWN), ("I32", 1.0)):
            act(r, mat(name), mat("ID"), AF.Identity, v)
        if r in WORKERS:
            iota(r, mat("JM"), [[0, 4], [1, 32]], 0, 0)
            cp(r, one("PF", 1), one("PI", 1))
            ts(r, mat("LB"), mat("JM"), one("PF", 1), 0.25, OP.is_equal, OP.mult)
            cp(r, mat("L16"), mat("LB"))
            act(r, mat("L32"), mat("LB"))
            ts(r, one("PF", 4), one("PI", 1), 4.0, 1.0, OP.mult, OP.add)
            ts(r, one("PF", 5), one("PI", 4), 0.0625, one("PF", 4), OP.mult, OP.add)
            ts(r, ap("FF", 0, 136), ap("JR", 0, 136), one("PF", 5), 0.25, OP.is_equal, OP.mult)

    for r in range(N):
        for src, stage, slot in ([("tb", "TD", 4)] if r == 0 else []) + [("x", "XD", r)]:
            moves = []
            for k, d in enumerate(WORKERS):
                rows = lambda a, b: ap(src, a, b, p0=32 * k, p1=32 * k + 32)
                if r == N - 1:
                    for a, b in zip(cuts, cuts[1:]):
                        dma(r, ap("XC", a, b) if d == r else ap(stage, a, b, lead=k), rows(4 * a, 4 * b), after=gates[r])
                    if d != r:
                        moves.append((d, ap("XC", 0, 512), ap(stage, 0, 512, lead=k)))
                elif d != r:
                    dma(r, ap(stage, 0, 512, lead=k), rows(0, W), after=gates[r])
                    moves.append((d, ap("XL", 0, 512, lead=slot), ap(stage, 0, 512, lead=k)))
            send(r, moves)
    for k, r in enumerate(WORKERS):
        first = gone(r)
        for slot, name, src, owner in [(4, "TB", "tb", 0)] + [(t, "XR%d" % t, "x", t) for t in range(4)]:
            for q in range(4):
                frm = ap(src, 0, W, p0=32 * k, p1=32 * k + 32) if owner == r else ap("XL", 0, 512, lead=slot)
                dma(r, ap(name, 0, W, p0=32 * q, p1=32 * q + 32), frm, after=first)

    loose, chooser = PAR["loose"], PAR["chooser"]
    blk = lambda name, m, s: ap(name, 128 * m + 64 * s, 128 * m + 64 * s + 64)
    col = lambda name, j, n=1: ap(name, 128 * j, 128 * (j + n))
    bit = lambda name, j, n=1: ap(name, 64 * j, 64 * (j + n))

    def four(r, kk, ps, sb, apart=False):
        for to, j, c, op in (("AA", 0, 0, OP.min), ("AA", 1, 0, OP.max), (ps, 2, 1, OP.min), (ps, 3, 1, OP.max)):
            for s in range(2 * apart):
                tt(r, blk(to, j, s), blk(ps, c, s), bit(kk, 4 * s + 2 * c), op)
            if not apart:
                tt(r, col(to, j), col(ps, c), col(kk, 2 * c), op)
        tt(r, col(sb, 0), col(ps, 2), col("AA", 0), OP.min)
        tt(r, col(ps, 0), col(ps, 3), col("AA", 1), OP.min)
        tt(r, col("AA", 2), col(ps, 2), col("AA", 0), OP.max)
        tt(r, col(sb, 3), col(ps, 3), col("AA", 1), OP.max)
        tt(r, col(sb, 2), col(ps, 0), col("AA", 2), OP.max)
        tt(r, col(sb, 1), col(ps, 0), col("AA", 2), OP.min)

    for r in range(N):
        kk, own, mix = "KK%d" % r, chooser[r] == r, pieces(PAR["mix"][r])
        nm = sum(v for p, v in mix if p == "M")
        for s in range(2):
            cp(r, blk("OFF", 0, s), blk("C0", 0, s))
        ts(r, mat("CK"), mat("C0"), float(BASE), 1 / DOWN, OP.add, OP.mult)
        for s in range(2):
            ts(r, ap("NB", 64 * s, 64 * s + 64 - nm), ap("ID", 0, 64 - nm), 0.0, -2047.0, OP.mult, OP.add)
            a, b = 1024 * s + 1024 - 16 * nm, 1024 * s + 1024
            act(r, ap("SQ", a, b), ap("X", a, b), AF.Square)
            mm(r, ap("PS%d" % s, 0, nm), [(ap("BB", 15 - p, 143 - p), ap("SQ", a + p, b, 16)) for p in range(16)])
            ts(r, ap("NB", 64 * s + 64 - nm, 64 * s + 64), ap("PS%d" % s, 0, nm), 1 / UP, -2047.0, OP.mult, OP.add)
        for m in range(5):
            ts(r, col("TF", m), col("TH", m), -1.0, 2048.0, OP.mult, OP.add)
            const(r, bit("KC", m), 3.0 * BASE + KEY * (4 * m - 1) - 2048)
        for m in range(5):
            for s in range(2):
                o, x0, u = 128 * m + 64 * s, 1024 * s, 0
                act(r, blk("HI", m, s), blk("CK", m, s), AF.Identity, 5 * DOWN, -4.0 * BASE - 5.0 * KEY * m - 1022.5)
                for p, n in mix:
                    a, b = x0 + 16 * u, x0 + 16 * (u + n)
                    src = ind(ap("TAB", 0, WIN if m else W), ap("OFF", o + u, o + u + n))
                    if p == "V":
                        tt(r, ap("DIFF", a, b), src, ap("X", a, b), OP.subtract)
                        act(r, ap("SQ", a, b), ap("DIFF", a, b), AF.Square)
                    else:
                        ps = ap("PS%d" % (2 + s), 0, 16 * n)
                        mm(r, ps, [(mat("N2"), ap("X", a, b))], end=False)
                        act(r, ap("GA", a, b), src)
                        mm(r, ps, [(mat("ID"), ap("GA", a, b))], more=True)
                        tt(r, ap("SQ", a, b), ps, ap("GA", a, b), OP.mult)
                    u += n
                d, ck = ap("PS%d" % s, 0, 64), blk("CK", m + 1, s) if m < 4 else blk(kk, 4, s)
                z, sb = ap("PS%d" % ((4, 7)[s] if r in loose else 4 + s), 0, 64), "PS%d" % (5 + s)
                mm(r, d, [(mat("U16"), blk("NB", 0, s)), (mat("P5"), blk("CK", m, s)), (mat("NU"), blk("HI", m, s))], end=False)
                mm(r, d, [(ap("BB", 15 - p, 143 - p), ap("SQ", x0 + p, x0 + 1024, 16)) for p in range(16)], more=True)
                zero = 2048.0 - 4.0 * BASE - 5.0 * KEY * m
                if m < 4:
                    ts(r, blk("OFF", m + 1, s), d, 1 / UP, zero, OP.mult, OP.add)
                act(r, ck, d, AF.Identity, 1 / (UP * DOWN), (zero + BASE + KEY * (m + 1)) / DOWN)
                pairs = [(mat("N5"), blk("CK", m, s)), (mat("PU"), blk("HI", m, s)), (mat("PU"), bit("KC", m)),
                         (mat("U16"), blk("TF", m, s)), (mat("UD"), ck)]
                if m == 4:
                    mm(r, z, pairs[:4], end=False)
                mm(r, z, pairs[4 * (m == 4):], more=m == 4)
                if r in loose:
                    tt(r, bit(sb, 4) if m % 2 else blk(kk, 5, s) if m == 4 else bit("AA", s), z, blk("CK", m, s), OP.max)
                    if m % 2:
                        tt(r, bit(sb, m // 2), bit(sb, 4), bit("AA", s), OP.min)
                        tt(r, bit("AA", 2 + s) if m == 1 else bit(sb, 5), bit(sb, 4), bit("AA", s), OP.max)
                    if m == 3:
                        tt(r, bit(sb, 2), bit(sb, 5), bit("AA", 2 + s), OP.min)
                        tt(r, bit(sb, 3), bit(sb, 5), bit("AA", 2 + s), OP.max)
                else:
                    tt(r, blk("PS7", m // 2, s) if m % 2 else blk(kk, m + (m == 4), s), z, blk("CK", m, s), OP.max)
                    if (m, s) == (3, 1):
                        four(r, kk, "PS7", "PS6" if own else kk)
                        if not own:
                            send(r, [(chooser[r], col(kk, 0, 4), col(kk, 0, 4))])
                    if (m, s) == (4, 1) and not own:
                        send(r, [(chooser[r], col(kk, 4, 2), col(kk, 4, 2))])

    def move(r, items):
        trip = [(ap(pb, c, c + n, p0=32 * q, p1=32 * q + 32), ap("D16", 32 * k, 32 * k + 32), ap(jh, a, a + n)) for pb, c, n, k, q, jh, a in items]

        def emit(g, T):
            for out, l, x in trip:
                last = g.tensor.matmul(real(T, out), real(T, l), real(T, x), True, True)
            return last
        return add(r, "P", emit, [a for v in trip for a in v[1:]], [v[0] for v in trip])

    def plain(r, jh, sb, a, b, c):
        act(r, ap("JK", c, c + b - a), ap(sb, a, b), AF.Identity, 1.0, -1023.5 / DOWN)
        tt(r, ap(jh, c, c + b - a), ap(sb, a, b), ap("JK", c, c + b - a), OP.subtract)

    def deal(t, pb, a, n, base):
        r = chooser[t]
        far = [k for k in range(4) if WORKERS[k] != r]
        js = lambda u, v: ap("JS", 512 * t + base + u, 512 * t + base + v)
        if far == list(range(far[0], far[-1] + 1)):
            cp(r, js(n * far[0], n * far[-1] + n), ap(pb, n * far[0], n * far[-1] + n))
        else:
            cp(r, js(0, 4 * n), ap(pb, 0, 4 * n))
        send(r, [(WORKERS[k], ap("OFT", 128 * t + a, 128 * t + a + n), js(n * k, n * k + n)) for k in far])
        for k in set(range(4)) - set(far):
            cp(r, ap("OFT", 128 * t + a, 128 * t + a + n), ap(pb, n * k, n * k + n))

    def quick(t, s, sb, pb):
        kk, jh = "KK%d" % t, "JH%d" % t
        n = PAR["ahead"][t][s]
        for j in range(4):
            tt(t, bit(sb, j), bit(sb, j), blk(kk, 4, s), OP.min)
        if n:
            act(t, bit("JK", 4 * s, n), bit(sb, 0, n), AF.Identity, 1.0, -1023.5 / DOWN)
        tt(t, bit(sb, 3), bit(sb, 3), blk(kk, 5, s), OP.min)
        if n:
            tt(t, bit(jh, 4 * s, n), bit(sb, 0, n), bit("JK", 4 * s, n), OP.subtract)
        plain(t, jh, sb, 64 * n, 256, 256 * s + 64 * n)
        for q in range(4):
            move(t, [(pb, 64 * k, 64, k, q, jh, 256 * s + 64 * q) for k in range(4)])
        deal(t, pb, 64 * s, 64, 256 * s)
        act(t, bit("KL%d" % t, 4 * s, 4), bit(sb, 0, 4))
        if t and s:
            send(t, [(0, col("KL%d" % t, 0, 4), col("KL%d" % t, 0, 4))])

    def late(t, sb, pb):
        r, kk, jh = chooser[t], "KK%d" % t, "JH%d" % t
        if r != t:
            mm(r, col(sb, 0, 4), [(mat("I32"), col(kk, 0, 4))])
        for j in range(4):
            tt(r, col(sb, j), col(sb, j), col(kk, 4), OP.min)
        for j in range(3):
            tt(r, col(kk, 6 + j), col(sb, j), col(kk, 5), OP.max)
        tt(r, col(sb, 0, 4), col(sb, 0, 4), col(kk, 5, 4), OP.min)
        plain(r, jh, sb, 0, 512, 0)
        for q in range(4):
            if t < N - 1:
                move(r, [(pb, 128 * k, 128, k, q, jh, 128 * q) for k in range(4)])
            else:
                move(r, [(pb, 128 * k + a // 4 + (b - a) // 8 * u, (b - a) // 8, k, q, jh, 128 * (2 * (q // 2) + u) + a // 4 + (b - a) // 8 * (q % 2))
                         for k in range(4) for a, b in zip(cuts, cuts[1:]) for u in range(2)])
        deal(t, pb, 0, 128, 0)

    outs = []
    for what in PAR["choose"].split():
        t, (sb, pb) = int(what[1]), ["PS" + v for v in what[-2:]]
        r, yj = chooser[t], ap("YJ%d" % t, 0, 512)
        if what[0] == "q":
            quick(t, int(what[2]), sb, pb)
            continue
        if what[0] == "l":
            late(t, sb, pb)
            mm(r, col(sb, 0, 4), [(mat("D16"), col("JH%d" % t, 0, 4))])
            act(r, yj, col(sb, 0, 4))
        else:
            r, kl = 0, "KL%d" % t
            for j in range(4):
                mm(r, bit(pb, j), [(mat("I32"), bit(kl, 4 * (j % 2) + j // 2 * 2 + 1))])
            four(r, kl, pb, sb, True)
            plain(r, "JL", sb, 0, 512, 0)
            act(r, yj, col("JL", 0, 4), AF.Identity, DOWN)
        if r != t:
            send(r, [(t, yj, yj)])
        outs.append((t, yj))

    def lists(t, a, b):
        return ap("OFT", 128 * t + a, 128 * t + b)

    def piece(k, b):
        return ap("ytau", 1024 * b, 1024 * b + 1024, p0=32 * k, p1=32 * k + 32)

    ready = {}

    def hand(r, names):
        send(r, [ready[(r, v)][:3] for v in names])
        for v in names:
            d, out, a, to = ready[(r, v)]
            dma(d, to, out, q="A" if d == N - 1 and to[2] // 32 % 2 else "S")

    for t, yj in outs:
        dma(t, ap("yj", 0, 512), yj)
    for t in range(4):
        for k, r in enumerate(WORKERS):
            win = ap("TB" if t == 0 else "T%d" % (t - 1), 0, W)
            b = 0
            for c, (how, n) in enumerate(pieces(PAR["steps"][t])):
                a, b = b, b + 64 * n
                src = ind(win, lists(t, a // 16, b // 16))
                ps = ap("PS" + (PAR["banks"][r][c] if t == 0 else str(c % 8)), 0, b - a)
                xr, out = ap("XR%d" % t, a, b), ap("T%d" % t, a, b)
                if how == "D":
                    gb = ap("G16" if t < 2 else "G32", a, b)
                    tt(r, gb, src, xr, OP.add)
                    pairs = [(mat("L16" if t < 2 else "L32"), gb)]
                elif how in "AB":
                    gb = ap("GH" if t == 0 else "G32", a, b)
                    act(r, gb, src)
                    pairs = [(mat("LB" if t == 0 else "L32"), gb)]
                else:
                    act(r, ap("GH", a, b), src)
                    tt(r, ap("GL", a, b), src, ap("GH", a, b), OP.subtract)
                    pairs = [(mat("LB"), ap("GH", a, b)), (mat("LB"), ap("GL", a, b))]
                if how in "BT":
                    mm(r, ps, [(mat("LB"), xr)], end=False)
                mm(r, ps, pairs, more=how in "BT")
                if how in "DBT":
                    act(r, out, ps)
                else:
                    tt(r, out, ps, xr, OP.add)
            for b in range(2):
                dma(r, piece(k, b) if r == t else ap("OD", 0, 256, lead=2 * t + b), ap("T%d" % t, 1024 * b, 1024 * b + 1024, p1=32))
                ready[(r, "ab"[b])] = (t, ap("LD", 0, 256, lead=2 * k + b), ap("OD", 0, 256, lead=2 * t + b), piece(k, b))
            if r != t and t < 3:
                hand(r, "ab")
    t, num = N - 1, 0
    for b, (c0, c1) in enumerate(zip(cuts, cuts[1:])):
        for k, r in enumerate(WORKERS):
            win, c, wd = ap("T3", 0, W), 0, c1 - c0
            for j, (how, n) in enumerate(pieces(PAR["fin"][b])):
                xc, ps = ap("XC", c0 + c, c0 + c + n), ap("PS%d" % (num + j), 0, n)
                pairs = [(mat("ID"), xc)] if how == "P" else []
                for jj in range(2):
                    a, lc = 2 * c0 + wd * jj + c, c0 // 4 + (wd * jj + c) // 16
                    ga, gv = ap("G32", a, a + n), ap("G32", 1024 + a, 1024 + a + n)
                    (cp if 2 * (num + j) + jj in PAR["solo"] else act)(r, ga, ind(win, lists(t, lc, lc + n // 16)))
                    tt(r, gv, ind(win, lists(t, lc + wd // 8, lc + wd // 8 + n // 16)), ga, OP.add)
                    mm(r, ps, pairs + [(ap("FF", 1 - jj, 129 - jj), gv)], more=jj == 1, end=jj == 1)
                    pairs = []
                fin = ap("FIN", c0 + c, c0 + c + n)
                if how == "P":
                    act(r, fin, ps)
                else:
                    tt(r, fin, ps, xc, OP.add)
                c += n
            to = ap("ytau", 4 * c0, 4 * c1, p0=32 * k, p1=32 * k + 32)
            ready[(r, "fghi"[b])] = (t, ap("L%d" % wd, 0, wd, lead=4 * b + k), ap("FIN", c0, c1), to)
            if r == t:
                dma(r, to, ap("FIN", c0, c1))
        num += len(pieces(PAR["fin"][b]))
    for r in WORKERS:
        for names in PAR["last"][r].split():
            hand(r, names)
    return nodes


def line_up(nodes):
    n = len(nodes)
    before = [set(v["deps"]) for v in nodes]
    for name, code in ORDER.items():
        rest, skip, last = [i for i, v in enumerate(nodes) if (v["r"], v["eng"]) == (int(name[0]), name[1])], 0, []
        for ch in code + "0" * len(rest):
            skip += LETTERS.index(ch)
            if rest and ch != LETTERS[-1]:
                i, skip = rest.pop(skip), 0
                before[i].update(last)
                last = [i]
    after = [[] for _ in range(n)]
    for i in range(n):
        for d in before[i]:
            after[d].append(i)
    left = [len(b) for b in before]
    seq = [i for i in range(n) if not left[i]]
    for i in seq:
        for u in after[i]:
            left[u] -= 1
            if not left[u]:
                seq.append(u)
    assert len(seq) == n
    return seq


def waits(nodes, seq):
    mark, count, place = {}, {}, {}
    for p, i in enumerate(seq):
        v = nodes[i]
        place[i] = p
        if v["sem"] is None:
            count[(v["r"], v["eng"])] = count.get((v["r"], v["eng"]), 0) + 1
            mark[i] = ("c" + v["eng"], count[(v["r"], v["eng"])])
        else:
            mark[i] = v["sem"]
    known, clock, need = {}, {}, {}
    for i in seq:
        v = nodes[i]
        if v["emit"] is None:
            clock[i] = {}
            continue
        k = known.setdefault((v["r"], v["eng"]), {})
        need[i] = {}
        for d in sorted(v["deps"], key=lambda d: -place[d]):
            name, c = mark[d]
            if name and k.get(name, 0) < c and not (v["eng"] == "P" and name == "cP"):
                need[i][name] = c
                k[name] = c
                for name2, c2 in clock[d].items():
                    k[name2] = max(k.get(name2, 0), c2)
        clock[i] = dict(k)
    return mark, need


PLAN = {}


def rank_program(g, core, T, topo):
    r = T.rank_of(core)
    if r is None:
        return
    if not PLAN:
        nodes = build(list(T.cores), topo)
        seq = line_up(nodes)
        PLAN["all"] = (nodes, seq) + waits(nodes, seq)
    nodes, seq, mark, need = PLAN["all"]
    queue = {"V": g.vector, "A": g.scalar, "P": g.tensor, "G": g, "S": g.sync}
    top, got = {}, {}
    for i, v in enumerate(nodes):
        if v["r"] == r and mark[i][0]:
            top[mark[i][0]] = max(top.get(mark[i][0], 0), mark[i][1])
    for i in seq:
        v = nodes[i]
        if v["r"] != r or not v["emit"]:
            continue
        for name, c in need[i].items():
            queue[v["eng"]].wait_ge(T.sem[name], c)
            got[name] = max(got.get(name, 0), c)
        ins = v["emit"](g, T)
        if ins is not None:
            name, c = v.get("inc", (mark[i][0], 1))
            ins.then_inc(T.sem[name], c)
    for name, c in top.items():
        if got.get(name, 0) < c:
            g.wait_ge(T.sem[name], c)
